import numpy as np, ml_dtypes
CORES = [16,18,20,22]
N = 4
import mx_ref
BF = ml_dtypes.bfloat16
def gentries(a):
    return np.ascontiguousarray(a.reshape(8, 16, -1).transpose(0, 2, 1)).reshape(8, -1)
def gtable(e):
    e = np.asarray(e); return np.ascontiguousarray(e.reshape(8, -1, 16).transpose(0, 2, 1)).reshape(128, -1).astype(np.int32)
def gcols(t, e):
    v = np.concatenate([t.reshape(8, 16, -1, 4), np.zeros((8, 16, 1, 4), BF)], axis=2)
    return np.ascontiguousarray(np.stack([v[g][:, e[g]] for g in range(8)])).reshape(128, -1)
def tile(rs):
    return np.stack(rs, axis=2).reshape(128, -1).astype(BF)
def pick(q, e):
    c = np.concatenate([q[0].reshape(128, -1, 4), np.zeros((128, 1, 4), np.uint8)], axis=1); s = np.concatenate([q[1], np.ones((16, 1), np.uint8)], axis=1)
    return (np.ascontiguousarray(c[:, e].reshape(128, -1)), np.ascontiguousarray(s[:, e]))
def join(*qs):
    return (np.concatenate([q[0] for q in qs], axis=1), np.concatenate([q[1] for q in qs], axis=1))
def put(q, e, v):
    c, s = q[0].reshape(128, -1, 4).copy(), q[1].copy(); c[:, e] = v[0].reshape(128, -1, 4); s[:, e] = v[1]
    return (c.reshape(128, -1), s)
def pk(c, s):
    return (np.ascontiguousarray(c), mx_ref.live(s))
def emit(q):
    return q[0], q[1]
def packed(v, rng):
    q = [mx_ref.quantize(np.ascontiguousarray(v[r])) for r in range(N)]
    return np.stack([a for a, b in q]), np.stack([mx_ref.plane(b, rng) for a, b in q])
def values_of_codes():
    e, c = np.zeros((128, 128, 4), np.float32), np.zeros((128, 2, 4), np.uint8)
    e[np.arange(128), np.arange(128), 0] = 1
    c[:127, :, 0] = np.arange(256).reshape(2, 128).T[:127]
    return mx_ref.matmul(mx_ref.quantize(e.reshape(128, 512).astype(BF)), (c.reshape(128, 8), np.full((16, 2), 127, np.uint8))).T.reshape(-1).astype(np.float64)
CODE_VALUE, SCALE_VALUE = values_of_codes(), 2.0 ** (np.arange(256) - 127.0)
def decode(q):
    return (CODE_VALUE[q[0]].reshape(16, 8, -1, 4) * SCALE_VALUE[q[1]][:, None, :, None] + 0.0).reshape(128, -1).astype(np.float32)
def f(rng, *shape):
    return mx_ref.flush((rng.standard_normal(shape, dtype=np.float32) * np.exp2(rng.integers(-2, 3, shape[:-1] + (1,)))).astype(BF))
def wide(rng, *shape, cols=0):
    v = rng.standard_normal(shape, dtype=np.float32) * np.exp2(rng.integers(-12, 13, shape)).astype(np.float32)
    if cols: v *= np.repeat(np.exp2(rng.integers(-cols, cols + 1, shape[:-2] + (1, shape[-1] // 4))) * (rng.random(shape[:-2] + (1, shape[-1] // 4)) > 0.0625), 4, axis=-1).astype(np.float32)
    return mx_ref.flush(v.astype(BF))
C, K, R = 320, 160, 3
def big(v):
    v = v.astype(np.float32)
    v[np.abs(v) < np.float32(2.0 ** -16)] = 0
    return v.astype(BF)
def numbers_of(rng):
    return {"x": np.array(f(rng, N, 128, 4 * C)), "u": np.array(f(rng, N, 128, 512)), "v": np.array(f(rng, N, 128, 512))}
def bindings(rng):
    return np.stack([gtable(np.argsort(rng.random((8, C)), axis=1)) for r in range(N)])
def targets(rng):
    return np.stack([gtable(rng.integers(0, C, (8, C))) for r in range(N)])
def layers(rng):
    return np.clip(f(rng, N, 128, 2048).astype(np.float32), -1.75, 1.75).astype(BF).reshape(N, 8, 16, 4, 8, 16, 4)
def planted(rng, quiet, pairs):
    w = layers(rng)
    w[:, :, :, :, :, quiet] = 0
    for a, b in pairs:
        for g in range(8): w[:, g, a, 0, g, b, 0] = 1
    return w
def weights(rng, w):
    c, p = packed(np.ascontiguousarray(w).reshape(N, 128, 2048), rng)
    return {"wc": c, "ws": p}
def setup_inputs(rng):
    return {**numbers_of(rng), "bd": bindings(rng), "ds": targets(rng), **weights(rng, layers(rng))}
def setup_inputs_ties(rng):
    d = numbers_of(rng)
    x = d["x"].reshape(N, 8, 16, C, 4)
    x[:, :, 0] = 0
    x[:, :, 0, :, 0] = rng.integers(-1, 2, (N, 8, C)).astype(np.float32).astype(BF)
    u = d["u"].reshape(N, 128, 128, 4)
    u[:, :, ::16] = 0
    o = rng.permutation(N)
    for r in range(N):
        for h in range(0, 128, 16): u[r, h + 1, h, 0] = 0.0 if r == o[0] else -1.0 if r == o[1] else 1.0
    return {"x": x.reshape(N, 128, 4 * C), "u": u.reshape(N, 128, 512), "v": d["v"], "bd": bindings(rng), "ds": targets(rng), **weights(rng, planted(rng, [0, 1], [(0, 1)]))}
def setup_inputs_near(rng):
    d = numbers_of(rng)
    x = d["x"].astype(np.float32).reshape(N, 8, 16, C, 4)
    x[:, :, :6] = 0
    x[:, :, 8:] = 0
    x[:, :, 0, :, 0] = 1
    x[:, :, 1, :, 0] = 1
    x[:, :, 4, :, 0] = rng.integers(-8, 9, (N, 8, C)) * 0.125
    x[:, :, 8, :, 0] = rng.integers(-8, 9, (N, 8, C)) * 2.0 ** -17
    u = d["u"].reshape(N, 128, 128, 4)
    u[:, :, ::16] = 0
    o = rng.permutation(N) % 4
    for r in range(N):
        c = np.where(rng.permutation(8) < 2, 1.0, -1.0)
        k = 1.0 if o[r] == 0 else 2.0 ** -12
        for h in range(0, 128, 16):
            if o[r] < 2:
                u[r, h + 2, h, 0] = c[h // 16] * k
                u[r, h + 3, h, 0] = c[h // 16] * k * 2.0 ** -10
                u[r, h + 10, h, 0] = k * 2.0 ** -4
            elif o[r] == 2:
                u[r, h + 10, h, 0] = 1.125 * 2.0 ** -30
                u[r, h + 11, h, 0] = -2.0 ** -30
            else:
                u[r, h + 5, h, 0] = 1.0
                u[r, h + 10, h, 0] = 1.0
    w = planted(rng, [0, 1, 2, 3, 4, 5, 8, 9, 10, 11, 12, 13, 14, 15], [(0, 2), (1, 3), (4, 5), (8, 10), (8, 11)])
    return {"x": x.reshape(N, 128, 4 * C).astype(BF), "u": u.reshape(N, 128, 512), "v": d["v"], "bd": bindings(rng), "ds": targets(rng), **weights(rng, w)}
def setup_inputs_ends(rng):
    d = numbers_of(rng)
    o = (np.arange(N) + rng.integers(N)) % N
    few = N // 4
    x = 2.0 ** 20 * (1 - 0.125 * rng.integers(0, 2, (N, 1, C, 1))) * np.ones((1, 128, 1, 4))
    c = 2.0 ** -30 * rng.choice([-1.0, 1.0], (128, 1, 4))
    less = rng.permutation(8) % 2 == 0
    u = d["u"].reshape(N, 128, 128, 4)
    v = rng.choice([-1.0, 1.0], (N, 128, 512))
    w = np.where(rng.random((N, 128, 512, 4)) < rng.random((N, 1, 512, 1)), 1.5, 1.75).reshape(N, 128, 2048)
    e, t = bindings(rng), np.zeros((N, 8, C), int)
    e[o[0]] = gtable(np.stack([np.arange(C)[::-1]] * 8))
    e[o[few]] = gtable(np.stack([np.arange(C)] * 8))
    for i in range(N):
        r = o[i]
        v[r] *= 2.0 ** 30 if i % 2 == 1 else 2.0 ** -30
        s = np.full(8, -1.0)
        if i == few:
            s = np.where(less, -1.0, 1.0)
            t[r][~np.roll(less, 1)] = C - 1
        u[r, :, ::16] = (s * (2.0 ** -30 if i < few else 2.0 ** 30)).astype(np.float32).astype(BF)[None, :, None]
        if i < few:
            x[r] = c
            t[r] = C - 1
            w[o[i + 1]] = 0
    return {"x": x.astype(np.float32).reshape(N, 128, 4 * C).astype(BF), "u": u.reshape(N, 128, 512), "v": v.astype(np.float32).astype(BF), "bd": e, "ds": np.stack([gtable(t[r]) for r in range(N)]), **weights(rng, w.astype(np.float32).astype(BF))}
def setup_inputs_odd(rng):
    d = numbers_of(rng)
    n = (N, 8, 16, C, 4)
    x = (1 + (2 * rng.integers(0, 64, n) + 1) * 2.0 ** -7) * np.exp2(-rng.integers(8, 15, n).astype(np.float64)) * rng.choice([-1.0, 1.0], n)
    x[:, :, ::8, :, 0] = rng.choice([1.96875, 1.875], (N, 8, 2, C))
    x[:, :, 9, :, 0] = 1.875
    x[:, :, 10, :, 0] = 0.09375
    x[:, :, 11, :, 0] = rng.integers(-15, 16, (N, 8, C)) * 0.125
    u = d["u"].reshape(N, 128, 128, 4)
    u[:, :, ::16] = 0
    for h in range(0, 128, 16): u[:, h + 13, h, 0] = 1.0
    w = planted(rng, [8, 9, 10, 11, 12, 13, 14, 15], [(9, 12), (10, 12), (11, 13)])
    for g in range(8): w[:, g, 11, 0, g, 13, 0] = 2.0 ** -12
    return {"x": x.astype(np.float32).reshape(N, 128, 4 * C).astype(BF), "u": u.reshape(N, 128, 512), "v": d["v"], "bd": bindings(rng), "ds": targets(rng), **weights(rng, w)}
def setup_inputs_spread(rng):
    d = setup_inputs(rng)
    d["x"] = big(wide(rng, N, 128, 4 * C, cols=4))
    return d
def check_inputs(d):
    b = []
    for k, m in (("x", 20), ("u", 30), ("v", 30)):
        a = np.abs(d[k].astype(np.float32))
        if not (np.isfinite(a).all() and ((a == 0) | (a >= 2.0 ** -30) & (a <= 2.0 ** m)).all()): b.append("a value of " + k)
    if not ((d["ds"] >= 0) & (d["ds"] < C)).all(): b.append("an entry of ds")
    none, least, most = [emit(mx_ref.quantize(np.full((128, 16), k, np.float32).astype(BF)))[1][0, 0] for k in (0.0, 2.0 ** -30, 1.75)]
    for r in range(N):
        if (np.sort(gentries(d["bd"][r]), axis=1) != np.arange(C)).any(): b.append("bd: not every port once in a group")
        if ((d["wc"][r] == 0x7F) | (d["wc"][r] == 0xFF)).any(): b.append("wc: a code that is no number")
        s = mx_ref.live(d["ws"][r])
        if ((s != none) & ((s < least) | (s > most))).any(): b.append("ws: a scale out of range")
        if (((d["wc"][r].reshape(16, 8, 512, 4) & 0x7F) != 0) & (s == none)[:, None, :, None]).any(): b.append("wc: a number other than zero at the scale of zeros")
        if not (np.abs(decode(pk(d["wc"][r], d["ws"][r]))) <= 1.75).all(): b.append("wc and ws: a number beyond 1.75 in size")
    return b
def reference(x, u, v, bd, ds, wc, ws):
    qu = [mx_ref.quantize(u[r]) for r in range(N)]
    lay = [pk(wc[r], ws[r]) for r in range(N)]
    now = [x[r] for r in range(N)]
    port = np.stack([gentries(bd[r]) for r in range(N)]).astype(np.int64)
    aim = np.stack([gentries(ds[r]) for r in range(N)]).astype(np.int64)
    for step in range(R):
        iv = np.argsort(port, axis=2)
        m = np.take_along_axis(iv, aim, axis=2)
        own = [decode(mx_ref.quantize(now[r])).astype(BF) for r in range(N)]
        z = [((own[r].astype(np.float32) + gcols(own[r], m[r]).astype(np.float32)) * np.float32(0.5)).astype(BF) for r in range(N)]
        out = [mx_ref.quantize(gcols(z[r], iv[r][:, K:])) for r in range(N)]
        reply = []
        for r in range(N):
            met = ((decode(out[(r - 1) % N]) + gcols(own[r], iv[r][:, :K]).astype(np.float32)) * np.float32(0.5)).astype(BF)
            q = mx_ref.quantize(met)
            reply.append(mx_ref.quantize(tile([mx_ref.matmul(pick(lay[r], np.arange(128 * b, 128 * b + 128)), q) * np.float32(0.0078125) for b in range(4)])))
        for r in range(N):
            q = reply[(r + 1) % N]
            back = gcols(decode(q).astype(BF), np.where(port[r] < K, -1, port[r] - K))
            now[r] = (z[r].astype(np.float32) + back.astype(np.float32)).astype(BF)
            s = mx_ref.matmul(qu[r], q)[::16] + np.float32(0.0)
            place = np.argsort(np.argsort(s, axis=1, kind="stable"), axis=1)
            for g in range(8):
                h = (g + 1) % 8
                k = np.nonzero(s[g] <= 0)[0]
                low, high = iv[r, h, place[g, k]], iv[r, h, K + k]
                port[r, h, low] = K + k
                port[r, h, high] = place[g, k]
    y, ob = np.zeros((N, 128, C), np.float32), np.zeros((N, 8, C), np.float32)
    oc, osc = np.zeros((N, 128, 4 * C), np.uint8), np.zeros((N, 16, C), np.uint8)
    for r in range(N):
        q = mx_ref.quantize(now[r])
        y[r] = mx_ref.matmul(mx_ref.quantize(v[r]), q)
        ob[r] = port[r]
        oc[r], osc[r] = emit(q)
    return {"y": y, "ob": ob, "oc": oc, "osc": osc}

@@ -1,0 +1,482 @@
+import numpy as np
+from concourse.mybir import dt, AluOpType, ActivationFunctionType
+
+C, K, R = 320, 160, 3
+KW = K // 16
+PL = C + K
+ROW = K + 1
+OFF = 240.0
+BIG = 1.0e29
+EARLY, MID, AMID, ND, ND_LAST, XAT, XAT_LAST, YAT = 2, 3, 0, 2, 3, 6, 6, 4
+ZM, ZG = 2, 3
+Q4, U8, BF, F32, I32, U16 = "float8_e4m3fn_x4", "uint8", "bfloat16", "float32", "int32", "uint16"
+
+SCRATCH = {"ps": ("psum", [128, 4096], F32)}
+
+
+def _sb(name, n, dtype):
+    SCRATCH[name] = ("sbuf", [128, n], dtype)
+
+
+def _pair(name, n):
+    _sb(name + "c", n, Q4)
+    _sb(name + "s", n, U8)
+
+
+_sb("one1", 520, BF), _sb("eye1", 520, BF), _sb("eyeh", 520, BF)
+_pair("eq1", 512), _pair("half", 512)
+_sb("pint", 2, I32), _sb("pand", 2, I32), _sb("pcol", 2, F32), _sb("ones", C, BF), _sb("iota", C, BF), _sb("r01", C, BF)
+_sb("jrow", C, BF), _sb("mask", C, BF), _sb("neg", K, F32), _sb("rneg", K, F32), _sb("kint", 16, F32), _sb("kk16", 16, F32)
+_sb("uint", 8, I32), _sb("uand", 8, I32), _sb("uoff", 8, U16), _sb("tini", C, BF), _sb("offc", 2, F32), _sb("rrow", 3 * ROW, BF)
+_sb("xs", 4 * C, BF), _sb("us", 512, BF), _sb("vs", 512, BF), _sb("bdi", 20, I32), _sb("dsi", 20, I32)
+_pair("lay", 512), _pair("qu", 128), _pair("qp", 128), _pair("qv", 128), _pair("qy", C)
+_sb("bdw", 20, U16), _sb("wtab", C, BF), _sb("pick", C, BF), _sb("run", C, BF), _sb("pick2", C, BF), _sb("run2", C, BF)
+_sb("bhi", KW, U16), _sb("blo", KW, U16), _sb("sig", C, BF), _sb("sig2", C, BF), _sb("portf", 20, F32), _sb("porth", 20, F32)
+_sb("portw", 20, U16), _sb("obw", 20, U16), _sb("obr", C, F32), _sb("trep0", C, BF), _sb("trep1", C, BF)
+for _r in range(R + 1):
+    _sb("tau%d" % _r, PL, BF), _sb("al%d" % _r, 20, U16)
+for _r in range(R):
+    _sb("tw%d" % _r, 20, U16)
+_sb("sm", K, F32), _sb("ss", K, F32), _sb("eq", K, BF), _sb("es", K, BF), _sb("sgn", 16, F32), _sb("keep", 16, F32), _sb("to", 16, F32)
+_sb("rows", KW * ROW, BF), _sb("rsum", 6 * ROW, BF), _sb("cnt", 16, F32)
+_sb("alo", 4 * K, BF), _sb("ahi", 4 * K, BF), _sb("mt", 4 * K, BF), _sb("vt", 4 * K, BF), _sb("ht", 4 * K, BF), _sb("xl", 4 * K, BF)
+_sb("xh", 4 * K, BF), _sb("xp", 4 * C, BF), _sb("xc", 4 * C, BF), _sb("yt", C, F32)
+for _r in range(R):
+    _sb("fh%d" % _r, 4 * C, BF)
+    for _n in ("m", "lm", "hh", "lh"):
+        _pair("%s%d" % (_n, _r), K)
+_pair("qm", K), _pair("ql", K), _pair("qh", K)
+
+SEMAPHORES = (["cv", "ca", "cp", "cg", "sent"] + ["am%d" % r for r in range(R)] + ["ah%d" % r for r in range(R)]
+              + ["d%d" % i for i in range(20)])
+
+
+def rank_program(g, core, T, topo):
+    rank = T.rank_of(core)
+    if rank is None:
+        return
+    n_ranks = len(T.cores)
+    nxt, prv = T.cores[(rank + 1) % n_ranks], T.cores[(rank - 1) % n_ranks]
+    A, ACT = AluOpType, ActivationFunctionType
+
+    queue = {"v": g.vector, "a": g.scalar, "p": g.tensor, "g": g, "s": g.sync}
+    own = {"v": "cv", "a": "ca", "p": "cp", "g": "cg"}
+    total = {}
+    known = {q: {} for q in queue}
+    events = []
+    last_w, last_r = {}, {}
+    n_dma = [0]
+
+    def cols(view):
+        name, a, b, st = view
+        if name not in last_w:
+            last_w[name] = np.full(SCRATCH[name][1][1], -1)
+            last_r[name] = {}
+        if name == "ps":
+            return slice(a // 512 * 512, (b + 511) // 512 * 512)
+        return slice(a, b, st)
+
+    def order(q, reads, writes):
+        deps = set()
+        for vw in reads:
+            s = cols(vw)
+            deps.update(last_w[vw[0]][s].tolist())
+            if vw[0] == "ps":
+                for sem, arr in last_r["ps"].items():
+                    if sem != own.get(q):
+                        deps.update(arr[s].tolist())
+        for vw in writes:
+            s = cols(vw)
+            deps.update(last_w[vw[0]][s].tolist())
+            for arr in last_r[vw[0]].values():
+                deps.update(arr[s].tolist())
+        deps.discard(-1)
+        for e in sorted(deps, reverse=True):
+            sem, n, clock = events[e]
+            if known[q].get(sem, 0) < n:
+                queue[q].wait_ge(T.sem[sem], n)
+                for k2, v2 in clock.items():
+                    known[q][k2] = max(known[q].get(k2, 0), v2)
+
+    def done(q, sem, inc, reads, writes):
+        total[sem] = total.get(sem, 0) + inc
+        clock = dict(known[q]) if q else {}
+        clock[sem] = total[sem]
+        events.append((sem, total[sem], clock))
+        e = len(events) - 1
+        for vw in reads:
+            s = cols(vw)
+            if sem not in last_r[vw[0]]:
+                last_r[vw[0]][sem] = np.full(SCRATCH[vw[0]][1][1], -1)
+            last_r[vw[0]][sem][s] = e
+        for vw in writes:
+            s = cols(vw)
+            last_w[vw[0]][s] = e
+
+    def call(q, reads, writes, make):
+        order(q, reads, writes)
+        make().then_inc(T.sem[own[q]], 1)
+        done(q, own[q], 1, reads, writes)
+
+    def dma(q, reads, writes, out, in_):
+        order(q, reads, writes)
+        sem = "d%d" % n_dma[0]
+        n_dma[0] += 1
+        queue[q].dma_start(out, in_).then_inc(T.sem[sem], 16)
+        done(q, sem, 16, reads, writes)
+
+    def V(name, a=0, b=None, st=1):
+        return (name, a, SCRATCH[name][1][1] if b is None else b, st)
+
+    def ap(vw):
+        name, a, b, st = vw
+        return T[name][:, a:b] if st == 1 else T[name][:, a:b:st]
+
+    def bank(i, n):
+        return V("ps", 512 * i, 512 * i + n)
+
+    def views(*xs):
+        return [x for x in xs if isinstance(x, tuple)]
+
+    def val(x):
+        return ap(x) if isinstance(x, tuple) else x
+
+    def src(x, off):
+        return ap(x) if off is None else ap(x).indirect(ap(off))
+
+    def memset(out, c):
+        call("v", [], [out], lambda: g.vector.memset(ap(out), c))
+
+    def copy(out, in_, off=None):
+        call("v", views(in_, off), [out], lambda: g.vector.tensor_copy(ap(out), src(in_, off)))
+
+    def scatter(win, off, in_):
+        call("v", [in_, off], [win], lambda: g.vector.tensor_copy(ap(win).indirect(ap(off)), ap(in_)))
+
+    def tt(out, a, b, op, off=None):
+        call("v", views(a, b, off), [out], lambda: g.vector.tensor_tensor(ap(out), src(a, off), ap(b), op))
+
+    def ts(out, a, s1, op0, s2=None, op1=None, off=None):
+        if op1 is None:
+            call("v", views(a, s1, off), [out], lambda: g.vector.tensor_scalar(ap(out), src(a, off), val(s1), None, op0))
+        else:
+            call("v", views(a, s1, s2, off), [out], lambda: g.vector.tensor_scalar(ap(out), src(a, off), val(s1), val(s2), op0, op1))
+
+    def scan(out, d0, d1, init, op0, op1):
+        call("v", [d0, d1], [out], lambda: g.vector.tensor_tensor_scan(ap(out), ap(d0), ap(d1), init, op0, op1))
+
+    def act(out, in_, func, off=None, bias=None, scale=None, acc=None):
+        kw = {}
+        if bias is not None:
+            kw["bias"] = val(bias)
+        if scale is not None:
+            kw["scale"] = val(scale)
+        if acc is not None:
+            kw["accum_out"] = ap(acc)
+        call("a", views(in_, off, bias, scale), views(out, acc), lambda: g.scalar.activation(ap(out), src(in_, off), func, **kw))
+
+    def quant(pair, in_, a=0):
+        n = (in_[2] - in_[1]) // 4
+        c, s = V(pair + "c", a, a + n), V(pair + "s", a, a + n)
+        call("v", [in_], [c, s], lambda: g.vector.quantize_mx(ap(c), ap(s), ap(in_)))
+
+    def mx(bk, w, a, x):
+        wc, ws, xc, xs = V(w + "c", a, a + 128), V(w + "s", a, a + 128), V(x + "c"), V(x + "s")
+        out = bank(bk, xc[2])
+        call("p", [wc, ws, xc, xs], [out], lambda: g.tensor.matmul_mx(ap(out), ap(wc), ap(ws), ap(xc), ap(xs), True, True))
+
+    def unpack(first, eye, x):
+        for b in range(4):
+            mx(first + b, eye, 128 * b, x)
+
+    def send(pair, land, dst, sem):
+        rid, pid, _ = topo.addr(dst)
+        m = topo.mask(core, dst)
+        order("g", [V(pair + "c"), V(pair + "s")], [])
+        g.remote_dma(T[land + "c"][:].bitcast(dt.uint8), T[pair + "c"][:].bitcast(dt.uint8), T.sem[sem], T.sem.sent, pid, rid, m)
+        g.remote_dma(T[land + "s"][:], T[pair + "s"][:], T.sem[sem], T.sem.sent, pid, rid, m)
+        total["sent"] = total.get("sent", 0) + 2 * len(topo.engines(core, dst))
+
+    def arrives(land, frm, sem):
+        done(None, sem, 2 * len(topo.engines(frm, core)), [], [V(land + "c"), V(land + "s")])
+
+    def unwrap(out, run, picked, n):
+        scan(V(run, 0, n), V("r01", 0, n), V(picked, 0, n), 0.0, A.mult, A.add)
+        ts(out, V(run, 15, n, 16), OFF, A.add)
+
+    def plane(name, b, a, z):
+        return V(name, C * b + a, C * b + z)
+
+    def quarter(name, b):
+        return V(name, K * b, K * b + K)
+
+    def elem(name, b, n):
+        return V(name, b, 4 * n, 4)
+
+    def evac(q, out, in_, c):
+        if q == "a":
+            act(out, in_, ACT.Copy, scale=c)
+        else:
+            ts(out, in_, c, A.mult)
+
+    for r in range(R):
+        arrives("lm%d" % r, prv, "am%d" % r)
+        arrives("lh%d" % r, nxt, "ah%d" % r)
+
+    dma("s", [], [V("bdi")], T.bdi[:], T.bd[:])
+    dma("s", [], [V("xs", 0, 4 * K)], T.xs[:, 0:4 * K], T.x[:, 0:4 * K])
+    dma("s", [], [V("xs", 4 * K, 4 * C)], T.xs[:, 4 * K:4 * C], T.x[:, 4 * K:4 * C])
+    dma("s", [], [V("dsi")], T.dsi[:], T.ds[:])
+    call("g", [], [V("pint")], lambda: g.iota(T.pint[:], [[0, 2]], 0, 1))
+    memset(V("one1"), 1.0)
+    call("g", [V("one1")], [V("eye1")], lambda: g.affine_select(T.eye1[:], T.one1[:], [[-1, 520]], A.is_equal, 0.0, 3, 4))
+    call("g", [], [V("kint")], lambda: g.iota(T.kint[:], [[16, 16]], K + 16, 0, allow_small_or_imprecise_dtypes=True))
+    call("g", [], [V("uint")], lambda: g.iota(T.uint[:], [[16, 8]], 112, 0))
+    memset(V("ones"), 1.0)
+    memset(V("r01"), 1.0)
+    ts(V("pand"), V("pint"), 15, A.bitwise_and)
+    scan(V("iota"), V("ones"), V("ones"), -OFF - 1.0, A.mult, A.add)
+    memset(V("r01", 0, C, 16), 0.0)
+    copy(V("pcol"), V("pand"))
+    scan(V("jrow"), V("r01"), V("r01"), 0.0, A.mult, A.add)
+    memset(V("tau0", 0, C), 0.0)
+    ts(V("mask"), V("jrow"), V("pcol", 0, 1), A.is_equal)
+    for b in range(4):
+        quant("eq1", V("eye1", 3 - b, 515 - b), 128 * b)
+    order("s", [V("xs")], [])
+    dma("s", [], [V("layc")], T.layc[:].bitcast(dt.uint8), T.wc[:])
+    dma("s", [], [V("lays")], T.lays[:], T.ws[:])
+    dma("s", [], [V("us")], T.us[:], T.u[:])
+    dma("s", [], [V("vs")], T.vs[:], T.v[:])
+
+    act(V("rrow"), V("one1", 0, 3 * ROW), ACT.Copy)
+    act(V("tini", 0, K), V("iota", 0, K), ACT.Copy)
+    act(V("rrow", 0, 3 * ROW, ROW), V("one1", 0, 3), ACT.Copy, scale=0.0)
+    act(V("tini", K, C), V("iota", K, C), ACT.Copy, bias=float(K))
+    act(V("offc"), V("one1", 0, 2), ACT.Copy, scale=OFF)
+    act(V("rneg"), V("r01", 0, K), ACT.Copy, scale=3 * BIG, bias=-3 * BIG)
+    act(V("neg"), V("mask", 0, K), ACT.Copy, scale=BIG, bias=-BIG)
+    act(V("eyeh"), V("eye1"), ACT.Copy, scale=0.5)
+    act(V("kk16"), V("kint"), ACT.Identity, bias=V("pcol", 0, 1))
+
+    def later_constants():
+        ts(V("uand"), V("uint"), 127, A.bitwise_and)
+        for b in range(4):
+            quant("half", V("eyeh", 3 - b, 515 - b), 128 * b)
+        copy(V("uoff"), V("uand"))
+
+    copy(V("bdw"), V("bdi"))
+    scatter(V("tau0", 0, C), V("bdw", 0, KW), V("iota", 0, K))
+    quant("ql", V("xs", 0, 4 * K))
+    unpack(4, "eq1", "ql")
+    scatter(V("tau0", 0, C), V("bdw", KW, 2 * KW), V("iota", K, C))
+    for b in range(4):
+        evac("a", plane("fh0", b, 0, K), bank(4 + b, K), 0.5)
+    tt(V("pick", 0, K), V("tau0", K, C), V("mask", 0, K), A.mult)
+    quant("qh", V("xs", 4 * K, 4 * C))
+    unpack(0, "eq1", "qh")
+    copy(V("tw0"), V("dsi"))
+    act(V("wtab"), V("tau0", 0, C), ACT.Copy, off=V("tw0"))
+    unwrap(V("al0", KW, 2 * KW), "run", "pick", K)
+    for b in range(3):
+        evac("v", plane("fh0", b, K, C), bank(b, K), 0.5)
+
+    def make_m(r):
+        fh, al = "fh%d" % r, "al%d" % r
+        hi = V(al, KW, 2 * KW)
+        tt(V("pick", 0, K), V("wtab"), V("mask", 0, K), A.mult, off=hi)
+        unwrap(V("bhi"), "run", "pick", K)
+        for b in range(4):
+            if r > 0 and b >= MID:
+                evac("a", plane(fh, b, K, C), bank(b, K), 0.5)
+            if r == 0 and b == 3:
+                evac("a", plane(fh, b, K, C), bank(b, K), 0.5)
+            if r == 0 or b >= AMID:
+                act(quarter("ahi", b), plane(fh, b, 0, C), ACT.Copy, off=hi)
+        for b in range(4):
+            tt(elem("mt", b, K), plane(fh, b, 0, C), quarter("ahi", b), A.add, off=V("bhi"))
+        quant("m%d" % r, V("mt"))
+        send("m%d" % r, "lm%d" % r, nxt, "am%d" % r)
+
+    def z_low(r, b):
+        out = elem("xl", b, K) if r < R - 1 else plane("xp", b, 0, K)
+        tt(out, plane("fh%d" % r, b, 0, C), quarter("alo", b), A.add, off=V("blo"))
+
+    def while_m_flies(r):
+        fh, al = "fh%d" % r, "al%d" % r
+        lo = V(al, 0, KW)
+        tt(V("pick", 0, K), V("tau%d" % r, 0, K), V("mask", 0, K), A.mult)
+        unwrap(lo, "run", "pick", K)
+        for b in range(4):
+            act(quarter("alo", b), plane(fh, b, 0, C), ACT.Copy, off=lo)
+        tt(V("pick2", 0, K), V("wtab"), V("mask", 0, K), A.mult, off=lo)
+        unwrap(V("blo"), "run2", "pick2", K)
+        if r == 0:
+            later_constants()
+            act(V("trep0"), V("tini"), ACT.Copy, off=V("tw0"))
+            act(V("trep1"), V("trep0"), ACT.Copy, off=V(al))
+        if r == R - 1:
+            act(V("sig"), V("iota"), ACT.Copy, off=V("al2"))
+            act(V("sig2"), V("sig"), ACT.Copy, off=V("al1"))
+        for b in range(ZM):
+            z_low(r, b)
+        if r == 0:
+            quant("qu", V("us"))
+            call("v", [V("quc"), V("uoff")], [V("qpc")], lambda: g.vector.tensor_copy(
+                T.qpc[:, 0:128].bitcast(dt.uint32), T.quc[:, 0:128].bitcast(dt.uint32).indirect(T.uoff[:, 0:8])))
+
+    def reply(r):
+        unpack(0, "half", "lm%d" % r)
+        for b in range(4):
+            tt(elem("vt", b, K), bank(b, K), quarter("alo", b), A.add)
+        quant("qm", V("vt"))
+        unpack(4, "lay", "qm")
+        for b in range(ZM, ZG):
+            z_low(r, b)
+        for b in range(4):
+            evac("av"[b % 2], elem("ht", b, K), bank(4 + b, K), 0.0078125)
+        quant("hh%d" % r, V("ht"))
+        send("hh%d" % r, "lh%d" % r, prv, "ah%d" % r)
+
+    def while_h_flies(r):
+        al = "al%d" % r
+        for b in range(ZG, 4):
+            z_low(r, b)
+        if r == 0:
+            call("a", [V("qus"), V("uoff")], [V("qps")], lambda: g.scalar.activation(
+                T.qps[:, 0:128], T.qus[:, 0:128].indirect(T.uoff[:, 0:8]), ACT.Copy))
+        act(V("tau%d" % (r + 1), 0, C), V("tini"), ACT.Copy)
+        if r < R - 1:
+            quant("ql", V("xl"))
+            unpack(4, "eq1", "ql")
+            for b in range(4):
+                evac("a", plane("fh%d" % (r + 1), b, 0, K), bank(4 + b, K), 0.5)
+            tt(V("pick2"), V("trep%d" % r), V("mask"), A.mult, off=V(al))
+            unwrap(V("tw%d" % (r + 1)), "run2", "pick2", C)
+        else:
+            quant("qv", V("vs"))
+            tt(V("pick2"), V("sig2"), V("mask"), A.mult, off=V("bdw"))
+            scan(V("run2"), V("r01"), V("pick2"), 0.0, A.mult, A.add)
+            ts(V("portf"), V("run2", 15, C, 16), OFF, A.add)
+            ts(V("portw"), V("run2", 15, C, 16), OFF, A.add)
+            ts(V("porth"), V("portf"), float(K), A.is_ge, float(K), A.mult)
+            tt(V("porth"), V("porth"), V("portf"), A.add)
+            copy(V("obw"), V("porth"))
+
+    def x_high(r, b):
+        out = elem("xh", b, K) if r < R - 1 else plane("xp", b, K, C)
+        tt(out, bank(b, K), elem("mt", b, K), A.add)
+
+    def x_col(q, b):
+        if q == "a":
+            act(elem("xc", b, C), plane("xp", b, 0, C), ACT.Copy, off=V("portw"))
+        else:
+            copy(elem("xc", b, C), plane("xp", b, 0, C), off=V("portw"))
+
+    def rebind(r):
+        last = r == R - 1
+        na = KW - (ND_LAST if last else ND)
+        lh, fh = "lh%d" % r, "fh%d" % (r + 1)
+        sv, sa = bank(4, K), bank(5, K)
+        mx(4, "qp", 0, lh)
+        mx(5, "qp", 0, lh)
+        unpack(0, "eq1", lh)
+
+        def own_score(c):
+            return V("ss", 16 * c + 15, 16 * c + 16)
+
+        def before(c):
+            ts(V("rows", ROW * c, ROW * c + 16 * c + 16), V("ps", sv[1], sv[1] + 16 * c + 16), own_score(c), A.is_le)
+
+        def after(c):
+            out = V("rows", ROW * c + 16 * c + 16, ROW * c + K)
+            if c < na:
+                act(out, V("ps", sa[1] + 16 * c + 16, sa[2]), ACT.Sign, bias=own_score(c), scale=-1.0)
+            elif c < KW - 1:
+                ts(out, V("ps", sv[1] + 16 * c + 16, sv[2]), own_score(c), A.is_lt)
+
+        def count(c):
+            act(V("rows", ROW * c, ROW * c + ROW), V("rows", ROW * c, ROW * c + ROW), ACT.Relu, acc=V("cnt", c, c + 1))
+
+        tt(V("sm"), sv, V("neg"), A.add)
+        scan(V("ss"), V("rneg"), V("sm"), 0.0, A.add, A.max)
+        for c in range(na):
+            after(c)
+        act(V("sgn", 0, KW), V("ss", 15, K, 16), ACT.Sign)
+        x_high(r, 0)
+        tt(V("eq"), sv, V("ss"), A.is_equal)
+        before(0)
+        scan(V("es"), V("r01", 0, K), V("eq"), 0.0, A.mult, A.add)
+        before(1)
+        ts(V("rows", K, KW * ROW, ROW), V("es", 15, K, 16), -1.0, A.mult, 16.0, A.add)
+        if not last:
+            for c in range(2, XAT):
+                before(c)
+            for b in range(1, 4):
+                x_high(r, b)
+            quant("qh", V("xh"))
+            unpack(0, "eq1", "qh")
+            for c in range(XAT, KW):
+                before(c)
+            for c in range(na):
+                count(c)
+            for b in range(EARLY):
+                evac("a", plane(fh, b, K, C), bank(b, K), 0.5)
+        else:
+            x_high(r, 1)
+            x_col("a", 0)
+            x_col("a", 1)
+            x_high(r, 2)
+            x_high(r, 3)
+            for c in range(2, XAT_LAST):
+                before(c)
+            x_col("v", 2)
+            x_col("v", 3)
+            quant("qy", V("xc"))
+            mx(6, "qv", 0, "qy")
+            dma("s", [V("qyc")], [], T.oc[:], T.qyc[:].bitcast(dt.uint8))
+            for k in range(4):
+                dma("s", [V("qys")], [], T.osc[4 * k:4 * k + 4, :], T.qys[32 * k:32 * k + 4, :])
+            for c in range(XAT_LAST, KW):
+                before(c)
+            for c in range(YAT):
+                count(c)
+            act(V("yt"), bank(6, C), ACT.Copy)
+            dma("s", [V("yt")], [], T.y[:], T.yt[:])
+            for c in range(YAT, na):
+                count(c)
+        for c in range(na, KW):
+            after(c)
+        n = ROW * (KW - na)
+        tt(V("keep", 0, KW), V("sgn", 0, KW), V("kk16", 0, KW), A.mult)
+        scan(V("rsum", 0, n), V("rrow", 0, n), V("rows", ROW * na, ROW * KW), 0.0, A.mult, A.add)
+        tt(V("to", 0, na), V("cnt", 0, na), V("keep", 0, na), A.max)
+        tt(V("to", na, KW), V("rsum", K, n, ROW), V("keep", na, KW), A.max)
+        hi = V("al%d" % (r + 1), KW, 2 * KW)
+        tau = "tau%d" % (r + 1)
+        ts(hi, V("to", 0, KW), -16.0, A.add)
+        scatter(V(tau, 0, C), hi, V("iota", K, C))
+        act(V(tau, C, PL), V("iota"), ACT.Copy, off=hi)
+        if not last:
+            tw = "tw%d" % (r + 1)
+            for b in range(EARLY, MID):
+                evac("a", plane(fh, b, K, C), bank(b, K), 0.5)
+            for b in range(AMID):
+                act(quarter("ahi", b), plane(fh, b, 0, C), ACT.Copy, off=hi)
+            copy(V("wtab", 0, K), V(tau), off=V(tw, 0, KW))
+            act(V("wtab", K, C), V(tau), ACT.Copy, off=V(tw, KW, 2 * KW))
+        else:
+            ts(V("obr", 0, K), V(tau), OFF, A.add, off=V("obw", 0, KW))
+            act(V("obr", K, C), V(tau), ACT.Identity, off=V("obw", KW, 2 * KW), bias=V("offc", 0, 1))
+            dma("s", [V("obr")], [], T.ob[:], T.obr[0:128:16, :])
+
+    for r in range(R):
+        make_m(r)
+        while_m_flies(r)
+        reply(r)
+        while_h_flies(r)
+        rebind(r)
+
+    for sem, n in total.items():
+        if known["g"].get(sem, 0) < n:
+            g.wait_ge(T.sem[sem], n)

@@ -1,13 +1,18 @@
 import numpy as np
-from concourse.mybir import dt, AluOpType, ActivationFunctionType
+from concourse.bass import DstId, RemoteDMATransfer
+from concourse.mybir import dt, AluOpType, AxisListType, ActivationFunctionType
 
 C, K, R = 320, 160, 3
 KW = K // 16
 PL = C + K
 ROW = K + 1
 OFF = 240.0
+FUSED, PC = False, 54
 BIG = 1.0e29
-EARLY, MID, AMID, ND, ND_LAST, XAT, XAT_LAST, YAT = 2, 3, 0, 2, 3, 6, 6, 4
+EARLY, MID, AMID, ND, ND_LAST, XAT, XAT_LAST, YAT = 2, 3, 0, 1, 1, 6, 10, 9
+TINY = 2.0 ** -20
+XA, BETA_FIRST = 3, True
+XCA, YPRE = 2, 0
 ZM, ZG = 2, 3
 Q4, U8, BF, F32, I32, U16 = "float8_e4m3fn_x4", "uint8", "bfloat16", "float32", "int32", "uint16"
 
@@ -23,11 +28,11 @@ def _pair(name, n):
     _sb(name + "s", n, U8)
 
 
-_sb("one1", 520, BF), _sb("eye1", 520, BF), _sb("eyeh", 520, BF)
-_pair("eq1", 512), _pair("half", 512)
+_sb("one1", 520, BF), _sb("eye1", 520, BF)
+_pair("eq1", 512)
 _sb("pint", 2, I32), _sb("pand", 2, I32), _sb("pcol", 2, F32), _sb("ones", C, BF), _sb("iota", C, BF), _sb("r01", C, BF)
 _sb("jrow", C, BF), _sb("mask", C, BF), _sb("neg", K, F32), _sb("rneg", K, F32), _sb("kint", 16, F32), _sb("kk16", 16, F32)
-_sb("uint", 8, I32), _sb("uand", 8, I32), _sb("uoff", 8, U16), _sb("tini", C, BF), _sb("offc", 2, F32), _sb("rrow", 3 * ROW, BF)
+_sb("uint", 8, I32), _sb("uand", 8, I32), _sb("uoff", 8, U16), _sb("tini", C, BF), _sb("offc", 2, F32), _sb("kkb", 16, F32), _sb("kkl", 16, F32)
 _sb("xs", 4 * C, BF), _sb("us", 512, BF), _sb("vs", 512, BF), _sb("bdi", 20, I32), _sb("dsi", 20, I32)
 _pair("lay", 512), _pair("qu", 128), _pair("qp", 128), _pair("qv", 128), _pair("qy", C)
 _sb("bdw", 20, U16), _sb("wtab", C, BF), _sb("pick", C, BF), _sb("run", C, BF), _sb("pick2", C, BF), _sb("run2", C, BF)
@@ -37,14 +42,17 @@ for _r in range(R + 1):
     _sb("tau%d" % _r, PL, BF), _sb("al%d" % _r, 20, U16)
 for _r in range(R):
     _sb("tw%d" % _r, 20, U16)
-_sb("sm", K, F32), _sb("ss", K, F32), _sb("eq", K, BF), _sb("es", K, BF), _sb("sgn", 16, F32), _sb("keep", 16, F32), _sb("to", 16, F32)
-_sb("rows", KW * ROW, BF), _sb("rsum", 6 * ROW, BF), _sb("cnt", 16, F32)
-_sb("alo", 4 * K, BF), _sb("ahi", 4 * K, BF), _sb("mt", 4 * K, BF), _sb("vt", 4 * K, BF), _sb("ht", 4 * K, BF), _sb("xl", 4 * K, BF)
-_sb("xh", 4 * K, BF), _sb("xp", 4 * C, BF), _sb("xc", 4 * C, BF), _sb("yt", C, F32)
+_sb("sm", K, F32), _sb("ss", K, F32), _sb("eq", K, BF), _sb("es", K, BF), _sb("pos", 16, F32), _sb("keep", 16, F32), _sb("wt", 16, F32)
+_sb("rows", KW * ROW, F32), _sb("cnt", 16, F32)
+_sb("alo", 4 * K, BF), _sb("ahi", 4 * K, BF), _sb("mt", 4 * K, BF), _sb("vt", 4 * K, BF), _sb("ht", 4 * K, BF), _sb("xg", 4 * K, BF)
+_sb("xt1", 4 * C, BF), _sb("xt2", 4 * C, BF), _sb("lo4", 4 * KW, U16), _pair("qg", K)
+_sb("xp", 4 * C, BF), _sb("xc", 4 * C, BF), _sb("yt", C, F32)
 for _r in range(R):
     _sb("fh%d" % _r, 4 * C, BF)
     for _n in ("m", "lm", "hh", "lh"):
-        _pair("%s%d" % (_n, _r), K)
+        _pair("%s%d" % (_n, _r), 256 if FUSED else K)
+if FUSED:
+    _sb("zero", 512, BF)
 _pair("qm", K), _pair("ql", K), _pair("qh", K)
 
 SEMAPHORES = (["cv", "ca", "cp", "cg", "sent"] + ["am%d" % r for r in range(R)] + ["ah%d" % r for r in range(R)]
@@ -180,10 +188,11 @@ def rank_program(g, core, T, topo):
         c, s = V(pair + "c", a, a + n), V(pair + "s", a, a + n)
         call("v", [in_], [c, s], lambda: g.vector.quantize_mx(ap(c), ap(s), ap(in_)))
 
-    def mx(bk, w, a, x):
-        wc, ws, xc, xs = V(w + "c", a, a + 128), V(w + "s", a, a + 128), V(x + "c"), V(x + "s")
+    def mx(bk, w, a, x, start=True, stop=True):
+        n = C if x == "qy" else K
+        wc, ws, xc, xs = V(w + "c", a, a + 128), V(w + "s", a, a + 128), V(x + "c", 0, n), V(x + "s", 0, n)
         out = bank(bk, xc[2])
-        call("p", [wc, ws, xc, xs], [out], lambda: g.tensor.matmul_mx(ap(out), ap(wc), ap(ws), ap(xc), ap(xs), True, True))
+        call("p", [wc, ws, xc, xs], [out], lambda: g.tensor.matmul_mx(ap(out), ap(wc), ap(ws), ap(xc), ap(xs), start, stop))
 
     def unpack(first, eye, x):
         for b in range(4):
@@ -193,12 +202,29 @@ def rank_program(g, core, T, topo):
         rid, pid, _ = topo.addr(dst)
         m = topo.mask(core, dst)
         order("g", [V(pair + "c"), V(pair + "s")], [])
-        g.remote_dma(T[land + "c"][:].bitcast(dt.uint8), T[pair + "c"][:].bitcast(dt.uint8), T.sem[sem], T.sem.sent, pid, rid, m)
-        g.remote_dma(T[land + "s"][:], T[pair + "s"][:], T.sem[sem], T.sem.sent, pid, rid, m)
-        total["sent"] = total.get("sent", 0) + 2 * len(topo.engines(core, dst))
+        eng = topo.engines(core, dst)
+        if FUSED:
+            n = len(eng) // 4
+            masks = [sum(1 << e for e in eng[i * n:i * n + n]) for i in range(4)]
+            to = [DstId(rid=rid, pnc=pid)]
+            ts_ = [RemoteDMATransfer(dst_ids=to, dma_engine_mask=masks[i], remote_sem=T.sem[sem],
+                                     src=T[pair + "c"][:, PC * i:PC * i + PC].bitcast(dt.uint8),
+                                     dst=T[land + "c"][:, PC * i:PC * i + PC].bitcast(dt.uint8)) for i in range(3)]
+            ts_.append(RemoteDMATransfer(dst_ids=to, dma_engine_mask=masks[3], remote_sem=T.sem[sem],
+                                         src=T[pair + "s"][:, 0:4 * PC], dst=T[land + "s"][:, 0:4 * PC]))
+            g.remote_dma_fused(ts_, local_sem=T.sem.sent)
+            total["sent"] = total.get("sent", 0) + len(eng)
+            return
+        g.remote_dma(T[land + "c"][:, 0:K].bitcast(dt.uint8), T[pair + "c"][:, 0:K].bitcast(dt.uint8), T.sem[sem], T.sem.sent, pid, rid, m)
+        g.remote_dma(T[land + "s"][:, 0:K], T[pair + "s"][:, 0:K], T.sem[sem], T.sem.sent, pid, rid, m)
+        total["sent"] = total.get("sent", 0) + 2 * len(eng)
 
     def arrives(land, frm, sem):
-        done(None, sem, 2 * len(topo.engines(frm, core)), [], [V(land + "c"), V(land + "s")])
+        done(None, sem, (1 if FUSED else 2) * len(topo.engines(frm, core)), [], [V(land + "c"), V(land + "s")])
+
+    def pad(pair):
+        if FUSED:
+            quant(pair, V("zero"), 128)
 
     def unwrap(out, run, picked, n):
         scan(V(run, 0, n), V("r01", 0, n), V(picked, 0, n), 0.0, A.mult, A.add)
@@ -225,8 +251,8 @@ def rank_program(g, core, T, topo):
 
     dma("s", [], [V("bdi")], T.bdi[:], T.bd[:])
     dma("s", [], [V("xs", 0, 4 * K)], T.xs[:, 0:4 * K], T.x[:, 0:4 * K])
-    dma("s", [], [V("xs", 4 * K, 4 * C)], T.xs[:, 4 * K:4 * C], T.x[:, 4 * K:4 * C])
     dma("s", [], [V("dsi")], T.dsi[:], T.ds[:])
+    dma("s", [], [V("xs", 4 * K, 4 * C)], T.xs[:, 4 * K:4 * C], T.x[:, 4 * K:4 * C])
     call("g", [], [V("pint")], lambda: g.iota(T.pint[:], [[0, 2]], 0, 1))
     memset(V("one1"), 1.0)
     call("g", [V("one1")], [V("eye1")], lambda: g.affine_select(T.eye1[:], T.one1[:], [[-1, 520]], A.is_equal, 0.0, 3, 4))
@@ -243,81 +269,103 @@ def rank_program(g, core, T, topo):
     ts(V("mask"), V("jrow"), V("pcol", 0, 1), A.is_equal)
     for b in range(4):
         quant("eq1", V("eye1", 3 - b, 515 - b), 128 * b)
+    if FUSED:
+        act(V("zero"), V("one1", 0, 512), ACT.Copy, scale=0.0)
+        pad("m0")
     order("s", [V("xs")], [])
     dma("s", [], [V("layc")], T.layc[:].bitcast(dt.uint8), T.wc[:])
     dma("s", [], [V("lays")], T.lays[:], T.ws[:])
     dma("s", [], [V("us")], T.us[:], T.u[:])
-    dma("s", [], [V("vs")], T.vs[:], T.v[:])
+    dma("s", [V("lh0c")], [V("vs")], T.vs[:], T.v[:])
 
-    act(V("rrow"), V("one1", 0, 3 * ROW), ACT.Copy)
     act(V("tini", 0, K), V("iota", 0, K), ACT.Copy)
-    act(V("rrow", 0, 3 * ROW, ROW), V("one1", 0, 3), ACT.Copy, scale=0.0)
     act(V("tini", K, C), V("iota", K, C), ACT.Copy, bias=float(K))
     act(V("offc"), V("one1", 0, 2), ACT.Copy, scale=OFF)
     act(V("rneg"), V("r01", 0, K), ACT.Copy, scale=3 * BIG, bias=-3 * BIG)
     act(V("neg"), V("mask", 0, K), ACT.Copy, scale=BIG, bias=-BIG)
-    act(V("eyeh"), V("eye1"), ACT.Copy, scale=0.5)
     act(V("kk16"), V("kint"), ACT.Identity, bias=V("pcol", 0, 1))
+    for name, nd in (("kkb", ND), ("kkl", ND_LAST)):
+        act(V(name, 0, KW - nd), V("kk16", 0, KW - nd), ACT.Copy, scale=1.0 / TINY)
+        act(V(name, KW - nd, 16), V("kk16", KW - nd, 16), ACT.Copy)
 
     def later_constants():
         ts(V("uand"), V("uint"), 127, A.bitwise_and)
-        for b in range(4):
-            quant("half", V("eyeh", 3 - b, 515 - b), 128 * b)
         copy(V("uoff"), V("uand"))
+        for name in ("hh0", "m1", "hh1", "m2", "hh2"):
+            pad(name)
 
     copy(V("bdw"), V("bdi"))
     scatter(V("tau0", 0, C), V("bdw", 0, KW), V("iota", 0, K))
     quant("ql", V("xs", 0, 4 * K))
     unpack(4, "eq1", "ql")
+    copy(V("tw0"), V("dsi"))
     scatter(V("tau0", 0, C), V("bdw", KW, 2 * KW), V("iota", K, C))
     for b in range(4):
         evac("a", plane("fh0", b, 0, K), bank(4 + b, K), 0.5)
-    tt(V("pick", 0, K), V("tau0", K, C), V("mask", 0, K), A.mult)
     quant("qh", V("xs", 4 * K, 4 * C))
     unpack(0, "eq1", "qh")
-    copy(V("tw0"), V("dsi"))
+    tt(V("pick", 0, K), V("tau0", K, C), V("mask", 0, K), A.mult)
     act(V("wtab"), V("tau0", 0, C), ACT.Copy, off=V("tw0"))
-    unwrap(V("al0", KW, 2 * KW), "run", "pick", K)
-    for b in range(3):
-        evac("v", plane("fh0", b, K, C), bank(b, K), 0.5)
+    scan(V("run", 0, K), V("r01", 0, K), V("pick", 0, K), 0.0, A.mult, A.add)
+    evac("v", plane("fh0", 0, K, C), bank(0, K), 0.5)
+    ts(V("al0", KW, 2 * KW), V("run", 15, K, 16), OFF, A.add)
+    evac("a", plane("fh0", 1, K, C), bank(1, K), 0.5)
 
     def make_m(r):
         fh, al = "fh%d" % r, "al%d" % r
         hi = V(al, KW, 2 * KW)
+        tau, lo, h = "tau%d" % r, V(al, 0, KW), K // 2
+        tt(V("pick2", 0, h), V(tau, 0, h), V("mask", 0, h), A.mult)
         tt(V("pick", 0, K), V("wtab"), V("mask", 0, K), A.mult, off=hi)
-        unwrap(V("bhi"), "run", "pick", K)
+        tt(V("pick2", h, K), V(tau, h, K), V("mask", h, K), A.mult)
+        scan(V("run", 0, K), V("r01", 0, K), V("pick", 0, K), 0.0, A.mult, A.add)
+        scan(V("run2", 0, K), V("r01", 0, K), V("pick2", 0, K), 0.0, A.mult, A.add)
+        ts(V("bhi"), V("run", 15, K, 16), OFF, A.add)
+        for b in range(2):
+            ts(V("lo4", KW * b, KW * b + KW), V("run2", 15, K, 16), 4.0, A.mult, 4 * OFF + b, A.add)
         for b in range(4):
             if r > 0 and b >= MID:
                 evac("a", plane(fh, b, K, C), bank(b, K), 0.5)
-            if r == 0 and b == 3:
+            if r == 0 and b == 1:
+                evac("a", plane(fh, 2, K, C), bank(2, K), 0.5)
+                evac("a", plane(fh, 3, K, C), bank(3, K), 0.5)
+            if False:
                 evac("a", plane(fh, b, K, C), bank(b, K), 0.5)
             if r == 0 or b >= AMID:
                 act(quarter("ahi", b), plane(fh, b, 0, C), ACT.Copy, off=hi)
         for b in range(4):
             tt(elem("mt", b, K), plane(fh, b, 0, C), quarter("ahi", b), A.add, off=V("bhi"))
+        ts(lo, V("run2", 15, K, 16), OFF, A.add)
+        for b in range(2, 4):
+            ts(V("lo4", KW * b, KW * b + KW), V("run2", 15, K, 16), 4.0, A.mult, 4 * OFF + b, A.add)
         quant("m%d" % r, V("mt"))
         send("m%d" % r, "lm%d" % r, nxt, "am%d" % r)
 
     def z_low(r, b):
-        out = elem("xl", b, K) if r < R - 1 else plane("xp", b, 0, K)
+        out = elem("xt%d" % (r + 1), b, K) if r < R - 1 else plane("xp", b, 0, K)
         tt(out, plane("fh%d" % r, b, 0, C), quarter("alo", b), A.add, off=V("blo"))
 
     def while_m_flies(r):
         fh, al = "fh%d" % r, "al%d" % r
         lo = V(al, 0, KW)
-        tt(V("pick", 0, K), V("tau%d" % r, 0, K), V("mask", 0, K), A.mult)
-        unwrap(lo, "run", "pick", K)
+        xt = V("xs" if r == 0 else "xt%d" % r)
+        for b in range(XA):
+            act(elem("xg", b, K), xt, ACT.Copy, off=V("lo4", KW * b, KW * b + KW))
+        for b in range(XA, 4):
+            copy(elem("xg", b, K), xt, off=V("lo4", KW * b, KW * b + KW))
+        if BETA_FIRST:
+            tt(V("pick2", 0, K), V("wtab"), V("mask", 0, K), A.mult, off=lo)
+        quant("qg", V("xg"))
+        for b in range(4):
+            mx(b, "eq1", 128 * b, "qg", True, False)
         for b in range(4):
             act(quarter("alo", b), plane(fh, b, 0, C), ACT.Copy, off=lo)
-        tt(V("pick2", 0, K), V("wtab"), V("mask", 0, K), A.mult, off=lo)
+        if not BETA_FIRST:
+            tt(V("pick2", 0, K), V("wtab"), V("mask", 0, K), A.mult, off=lo)
         unwrap(V("blo"), "run2", "pick2", K)
         if r == 0:
             later_constants()
             act(V("trep0"), V("tini"), ACT.Copy, off=V("tw0"))
-            act(V("trep1"), V("trep0"), ACT.Copy, off=V(al))
-        if r == R - 1:
-            act(V("sig"), V("iota"), ACT.Copy, off=V("al2"))
-            act(V("sig2"), V("sig"), ACT.Copy, off=V("al1"))
         for b in range(ZM):
             z_low(r, b)
         if r == 0:
@@ -326,10 +374,15 @@ def rank_program(g, core, T, topo):
                 T.qpc[:, 0:128].bitcast(dt.uint32), T.quc[:, 0:128].bitcast(dt.uint32).indirect(T.uoff[:, 0:8])))
 
     def reply(r):
-        unpack(0, "half", "lm%d" % r)
         for b in range(4):
-            tt(elem("vt", b, K), bank(b, K), quarter("alo", b), A.add)
+            mx(b, "eq1", 128 * b, "lm%d" % r, False, True)
+        for b in range(4):
+            evac("av"[b % 2], elem("vt", b, K), bank(b, K), 0.5)
         quant("qm", V("vt"))
+        if r == 0:
+            act(V("trep1"), V("trep0"), ACT.Copy, off=V("al0"))
+        if r == R - 1:
+            act(V("sig"), V("iota"), ACT.Copy, off=V("al2"))
         unpack(4, "lay", "qm")
         for b in range(ZM, ZG):
             z_low(r, b)
@@ -345,9 +398,11 @@ def rank_program(g, core, T, topo):
         if r == 0:
             call("a", [V("qus"), V("uoff")], [V("qps")], lambda: g.scalar.activation(
                 T.qps[:, 0:128], T.qus[:, 0:128].indirect(T.uoff[:, 0:8]), ACT.Copy))
+        if r == R - 1:
+            act(V("sig2"), V("sig"), ACT.Copy, off=V("al1"))
         act(V("tau%d" % (r + 1), 0, C), V("tini"), ACT.Copy)
         if r < R - 1:
-            quant("ql", V("xl"))
+            quant("ql", V("xt%d" % (r + 1), 0, 4 * K))
             unpack(4, "eq1", "ql")
             for b in range(4):
                 evac("a", plane("fh%d" % (r + 1), b, 0, K), bank(4 + b, K), 0.5)
@@ -357,14 +412,11 @@ def rank_program(g, core, T, topo):
             quant("qv", V("vs"))
             tt(V("pick2"), V("sig2"), V("mask"), A.mult, off=V("bdw"))
             scan(V("run2"), V("r01"), V("pick2"), 0.0, A.mult, A.add)
-            ts(V("portf"), V("run2", 15, C, 16), OFF, A.add)
+            ts(V("porth"), V("run2", 15, C, 16), K - OFF, A.is_ge, float(K), A.mult)
             ts(V("portw"), V("run2", 15, C, 16), OFF, A.add)
-            ts(V("porth"), V("portf"), float(K), A.is_ge, float(K), A.mult)
-            tt(V("porth"), V("porth"), V("portf"), A.add)
-            copy(V("obw"), V("porth"))
 
     def x_high(r, b):
-        out = elem("xh", b, K) if r < R - 1 else plane("xp", b, K, C)
+        out = V("xt%d" % (r + 1), 4 * K + b, 4 * C, 4) if r < R - 1 else plane("xp", b, K, C)
         tt(out, bank(b, K), elem("mt", b, K), A.add)
 
     def x_col(q, b):
@@ -379,59 +431,90 @@ def rank_program(g, core, T, topo):
         lh, fh = "lh%d" % r, "fh%d" % (r + 1)
         sv, sa = bank(4, K), bank(5, K)
         mx(4, "qp", 0, lh)
+        mx(0, "eq1", 0, lh)
         mx(5, "qp", 0, lh)
-        unpack(0, "eq1", lh)
+        for b in range(1, 4):
+            mx(b, "eq1", 128 * b, lh)
 
         def own_score(c):
             return V("ss", 16 * c + 15, 16 * c + 16)
 
+        def row(c):
+            return V("rows", ROW * c, ROW * c + ROW)
+
         def before(c):
-            ts(V("rows", ROW * c, ROW * c + 16 * c + 16), V("ps", sv[1], sv[1] + 16 * c + 16), own_score(c), A.is_le)
+            out, in_ = V("rows", ROW * c, ROW * c + 16 * c + 16), V("ps", sv[1], sv[1] + 16 * c + 16)
+            if c < na:
+                ts(out, in_, own_score(c), A.is_le)
+            else:
+                ts(out, in_, own_score(c), A.is_le, V("wt", c, c + 1), A.mult)
 
         def after(c):
             out = V("rows", ROW * c + 16 * c + 16, ROW * c + K)
+            if c == KW - 1:
+                return
             if c < na:
                 act(out, V("ps", sa[1] + 16 * c + 16, sa[2]), ACT.Sign, bias=own_score(c), scale=-1.0)
-            elif c < KW - 1:
-                ts(out, V("ps", sv[1] + 16 * c + 16, sv[2]), own_score(c), A.is_lt)
+            else:
+                ts(out, V("ps", sv[1] + 16 * c + 16, sv[2]), own_score(c), A.is_lt, V("wt", c, c + 1), A.mult)
 
         def count(c):
-            act(V("rows", ROW * c, ROW * c + ROW), V("rows", ROW * c, ROW * c + ROW), ACT.Relu, acc=V("cnt", c, c + 1))
+            if c < na:
+                act(row(c), row(c), ACT.Relu, scale=V("wt", c, c + 1), acc=V("cnt", c, c + 1))
+            else:
+                call("v", [row(c)], [V("cnt", c, c + 1)], lambda: g.vector.tensor_reduce(T.cnt[:, c:c + 1], ap(row(c)), AxisListType.X, A.add))
 
+        mine = V("ss", 15, K, 16)
         tt(V("sm"), sv, V("neg"), A.add)
+        x_high(r, 0)
         scan(V("ss"), V("rneg"), V("sm"), 0.0, A.add, A.max)
         for c in range(na):
             after(c)
-        act(V("sgn", 0, KW), V("ss", 15, K, 16), ACT.Sign)
-        x_high(r, 0)
-        tt(V("eq"), sv, V("ss"), A.is_equal)
+        x_high(r, 1)
+        tt(V("eq"), sv, V("ss"), A.not_equal)
+        ts(V("pos", 0, KW), mine, 0.0, A.is_gt)
+        ts(V("wt", 0, KW), mine, 0.0, A.is_le, TINY, A.max)
         before(0)
         scan(V("es"), V("r01", 0, K), V("eq"), 0.0, A.mult, A.add)
+        tt(V("keep", 0, KW), V("pos", 0, KW), V("kkl" if last else "kkb", 0, KW), A.mult)
         before(1)
-        ts(V("rows", K, KW * ROW, ROW), V("es", 15, K, 16), -1.0, A.mult, 16.0, A.add)
+        before(2)
+        tt(V("rows", K, na * ROW, ROW), V("es", 15, 16 * na, 16), V("keep", 0, na), A.add)
+        before(3)
+        for c in range(na, KW):
+            ts(V("rows", ROW * c + K, ROW * c + ROW), V("es", 16 * c + 15, 16 * c + 16), V("wt", c, c + 1), A.mult, V("keep", c, c + 1), A.add)
         if not last:
-            for c in range(2, XAT):
+            for c in range(4, XAT):
                 before(c)
-            for b in range(1, 4):
-                x_high(r, b)
-            quant("qh", V("xh"))
+            x_high(r, 2)
+            x_high(r, 3)
+            before(XAT)
+            before(XAT + 1)
+            quant("qh", V("xt%d" % (r + 1), 4 * K, 4 * C))
             unpack(0, "eq1", "qh")
-            for c in range(XAT, KW):
+            for c in range(XAT + 2, KW):
                 before(c)
             for c in range(na):
                 count(c)
             for b in range(EARLY):
                 evac("a", plane(fh, b, K, C), bank(b, K), 0.5)
         else:
-            x_high(r, 1)
             x_col("a", 0)
             x_col("a", 1)
             x_high(r, 2)
             x_high(r, 3)
-            for c in range(2, XAT_LAST):
+            for c in range(YPRE):
+                count(c)
+            if XCA == 3:
+                x_col("a", 2)
+            for c in range(4, XAT_LAST - 1):
                 before(c)
-            x_col("v", 2)
+            tt(V("portf"), V("porth"), V("run2", 15, C, 16), A.add)
+            if XCA == 2:
+                x_col("v", 2)
+            ts(V("obw"), V("portf"), OFF, A.add)
             x_col("v", 3)
+            before(XAT_LAST - 1)
             quant("qy", V("xc"))
             mx(6, "qv", 0, "qy")
             dma("s", [V("qyc")], [], T.oc[:], T.qyc[:].bitcast(dt.uint8))
@@ -439,7 +522,7 @@ def rank_program(g, core, T, topo):
                 dma("s", [V("qys")], [], T.osc[4 * k:4 * k + 4, :], T.qys[32 * k:32 * k + 4, :])
             for c in range(XAT_LAST, KW):
                 before(c)
-            for c in range(YAT):
+            for c in range(YPRE, YAT):
                 count(c)
             act(V("yt"), bank(6, C), ACT.Copy)
             dma("s", [V("yt")], [], T.y[:], T.yt[:])
@@ -447,14 +530,11 @@ def rank_program(g, core, T, topo):
                 count(c)
         for c in range(na, KW):
             after(c)
-        n = ROW * (KW - na)
-        tt(V("keep", 0, KW), V("sgn", 0, KW), V("kk16", 0, KW), A.mult)
-        scan(V("rsum", 0, n), V("rrow", 0, n), V("rows", ROW * na, ROW * KW), 0.0, A.mult, A.add)
-        tt(V("to", 0, na), V("cnt", 0, na), V("keep", 0, na), A.max)
-        tt(V("to", na, KW), V("rsum", K, n, ROW), V("keep", na, KW), A.max)
+        for c in reversed(range(na, KW)):
+            count(c)
         hi = V("al%d" % (r + 1), KW, 2 * KW)
         tau = "tau%d" % (r + 1)
-        ts(hi, V("to", 0, KW), -16.0, A.add)
+        ts(hi, V("cnt", 0, KW), -15.75, A.add)
         scatter(V(tau, 0, C), hi, V("iota", K, C))
         act(V(tau, C, PL), V("iota"), ACT.Copy, off=hi)
         if not last:

@@ -1,20 +1,28 @@
 import numpy as np
-from concourse.bass import DstId, RemoteDMATransfer
 from concourse.mybir import dt, AluOpType, AxisListType, ActivationFunctionType
 
 C, K, R = 320, 160, 3
 KW = K // 16
 PL = C + K
-ROW = K + 1
 OFF = 240.0
-FUSED, PC = False, 54
 BIG = 1.0e29
-EARLY, MID, AMID, ND, ND_LAST, XAT, XAT_LAST, YAT = 2, 3, 0, 1, 1, 6, 10, 9
+DROP = 512.0
+ROW = K + 4
 TINY = 2.0 ** -20
-XA, BETA_FIRST = 3, True
-XCA, YPRE = 2, 0
-ZM, ZG = 2, 3
 Q4, U8, BF, F32, I32, U16 = "float8_e4m3fn_x4", "uint8", "bfloat16", "float32", "int32", "uint16"
+
+PLACES = ("sm x0 ss s1.a s3.a s2.a s0.a x1 ne gt s6.a wt b0 s5.a s4.a es keep n0 b2 n2 b8 b1 n1 x3 b3 n3 s8.v n8 b4 n4 b7 b5 n5 x2 t9 b6 n6 "
+          "s7.v b9 n7 qx e0.a n9 hi tau.a e1.a sc w1.a w0.v lp bp ls e3.a a0.a bs e2.a l0 a1.a l1 bhi a2.a lo m0 a3.a m1 m2 g0.a m3 l3 g1.a l2 "
+          "y0.a qm g2.a y2.a g3.v zp qg y1.a zs blo z0 z1 ")
+OPT = dict(
+    pe=(False, False, True), nd=1, parts=1, slot=(0, 1, 2),
+    p0="eye0 first pand tau0 pcol mask.a r01 eye E3 E0 bd E2 sc ds w0.a w1.a Q0 F0.a F3.a E1 hp Q1 hs hi F2.v F4.a F1.a bp a0.a F5.v bs F6.a "
+       "a2.a early F7.v a3.a bhi a1.v m0 m1 trep0.a m2 m3 qm lp uoff neg ls lo l1 l2 l3 g2.a l0 g1.v g3.v g0.a y1.a y0.a zp y3.a qg zs blo qu "
+       "y2.a z1 z0 v0.a v1.v v2.a v3.v qv h0.a h2.a z2 z3 ps wide.a tr.a rneg h1.v h3.v qh late0 pc ql f0.a f1.a f2.a f3.a tp kk ts tw",
+    p1=PLACES + "v0.a v1.v v2.a v3.v y3.a qv h0.a h2.a qf2 z2 h1.v h3.v qh z3 ql f0.a f2.a tp f1.a qf1 f3.a ts tw late1",
+    p2=PLACES + "sig.a v0.a v1.v v2.a v3.v y3.a sig2.a qv h0.a z3 h2.a z2 h1.v h3.v qh pp tab pn bk ph pw pf qV ow",
+    p3="x2 G2.a sm x3 G3.a x1 ss pos.v x0 G0.a eq z c1.v G1.a c0.v nwt c6.v c9.v wb r6 r9 c4.v c5.v c3.v r3 c8.v r1 c2.v r2 c7.v r7 r5 q0 r8 r4 "
+       "q1 q2 qy0 yt0.a min scan hi sc tau.a o0 o1")
 
 SCRATCH = {"ps": ("psum", [128, 4096], F32)}
 
@@ -23,40 +31,80 @@ def _sb(name, n, dtype):
     SCRATCH[name] = ("sbuf", [128, n], dtype)
 
 
+PART = {}
+
+
+def _shared(host, n, dtype, names):
+    for k, name in enumerate(names.split()):
+        PART[name] = (host, n * k, n)
+    _sb(host, n * len(names.split()), dtype)
+
+
 def _pair(name, n):
     _sb(name + "c", n, Q4)
     _sb(name + "s", n, U8)
 
 
-_sb("one1", 520, BF), _sb("eye1", 520, BF)
-_pair("eq1", 512)
-_sb("pint", 2, I32), _sb("pand", 2, I32), _sb("pcol", 2, F32), _sb("ones", C, BF), _sb("iota", C, BF), _sb("r01", C, BF)
-_sb("jrow", C, BF), _sb("mask", C, BF), _sb("neg", K, F32), _sb("rneg", K, F32), _sb("kint", 16, F32), _sb("kk16", 16, F32)
-_sb("uint", 8, I32), _sb("uand", 8, I32), _sb("uoff", 8, U16), _sb("tini", C, BF), _sb("offc", 2, F32), _sb("kkb", 16, F32), _sb("kkl", 16, F32)
+_sb("one1", 520, BF), _sb("eye1", 520, BF), _sb("blk1", 512, BF), _sb("blk2", 512, BF)
+_pair("eq1", 512), _pair("bk", 128)
+_sb("pint", 2, I32), _sb("pand", 2, I32), _sb("pcol", 2, F32), _sb("diag", 128, BF), _sb("iota", C, BF), _sb("r01", C, BF)
+_sb("jrow", K, BF), _sb("wtab", C, BF), _sb("mask", C, BF), _sb("neg", K, F32), _sb("rneg", K, F32), _sb("port", K, F32), _sb("tab", K, F32), _sb("cb", 16, F32)
+_sb("uint", 8, I32), _sb("uand", 8, I32), _sb("uoff", 8, U16), _sb("offc", 2, F32)
 _sb("xs", 4 * C, BF), _sb("us", 512, BF), _sb("vs", 512, BF), _sb("bdi", 20, I32), _sb("dsi", 20, I32)
 _pair("lay", 512), _pair("qu", 128), _pair("qp", 128), _pair("qv", 128), _pair("qy", C)
-_sb("bdw", 20, U16), _sb("wtab", C, BF), _sb("pick", C, BF), _sb("run", C, BF), _sb("pick2", C, BF), _sb("run2", C, BF)
+_sb("bdw", 20, U16), _sb("pick", 4 * C, BF), _sb("run", 4 * C, BF)
 _sb("bhi", KW, U16), _sb("blo", KW, U16), _sb("sig", C, BF), _sb("sig2", C, BF), _sb("portf", 20, F32), _sb("porth", 20, F32)
-_sb("portw", 20, U16), _sb("obw", 20, U16), _sb("obr", C, F32), _sb("trep0", C, BF), _sb("trep1", C, BF)
+_sb("portw", 20, U16), _sb("obw", 20, U16), _sb("obr", C, F32), _sb("tw0", 20, U16), _sb("tw1", 20, U16), _sb("tw2", 20, U16), _sb("tini", C, BF)
 for _r in range(R + 1):
     _sb("tau%d" % _r, PL, BF), _sb("al%d" % _r, 20, U16)
 for _r in range(R):
-    _sb("tw%d" % _r, 20, U16)
-_sb("sm", K, F32), _sb("ss", K, F32), _sb("eq", K, BF), _sb("es", K, BF), _sb("pos", 16, F32), _sb("keep", 16, F32), _sb("wt", 16, F32)
-_sb("rows", KW * ROW, F32), _sb("cnt", 16, F32)
-_sb("alo", 4 * K, BF), _sb("ahi", 4 * K, BF), _sb("mt", 4 * K, BF), _sb("vt", 4 * K, BF), _sb("ht", 4 * K, BF), _sb("xg", 4 * K, BF)
+    _sb("trep%d" % _r, C, BF)
+_shared("score", K, F32, "sm ss col cnt sg arow"), _shared("few", 16, F32, "nwt wb sum wt"), _sb("eq", K, BF)
+_sb("fl", 12 * K, BF), _pair("qf", 3 * K), _sb("rest", KW * K, F32), _sb("rows", K * ROW, BF)
+_shared("kk", 16, F32, "kint kkb")
+_sb("fp", 4 * C, BF), _sb("alo", 4 * K, BF), _sb("ahi", 4 * K, BF), _sb("mt", 4 * K, BF), _sb("vt", 4 * K, BF), _sb("ht", 4 * K, BF), _sb("xg", 4 * K, BF)
 _sb("xt1", 4 * C, BF), _sb("xt2", 4 * C, BF), _sb("lo4", 4 * KW, U16), _pair("qg", K)
 _sb("xp", 4 * C, BF), _sb("xc", 4 * C, BF), _sb("yt", C, F32)
 for _r in range(R):
     _sb("fh%d" % _r, 4 * C, BF)
     for _n in ("m", "lm", "hh", "lh"):
-        _pair("%s%d" % (_n, _r), 256 if FUSED else K)
-if FUSED:
-    _sb("zero", 512, BF)
+        _pair("%s%d" % (_n, _r), K)
 _pair("qm", K), _pair("ql", K), _pair("qh", K)
 
 SEMAPHORES = (["cv", "ca", "cp", "cg", "sent"] + ["am%d" % r for r in range(R)] + ["ah%d" % r for r in range(R)]
-              + ["d%d" % i for i in range(20)])
+              + ["d%d" % i for i in range(24)])
+
+
+def cols(view):
+    name, a, b, st = view
+    if name == "ps":
+        return slice(a // 512 * 512, (b + 511) // 512 * 512)
+    return slice(a, b, st)
+
+
+def deal(calls):
+    n = len(calls)
+    turn = [c["turn"] for c in calls]
+    for i, c in enumerate(calls):
+        if turn[i] is None and c["q"] in ("s", "g", "p") and not any(calls[d]["kind"] == "land" for d in c["deps"] if c["q"] == "p"):
+            turn[i] = max([turn[d] for d in c["deps"] if turn[d] is not None] + [-1])
+    users = [[] for _ in calls]
+    for i in reversed(range(n)):
+        if turn[i] is None:
+            turn[i] = min([turn[j] for j in users[i]])
+        for d in calls[i]["deps"]:
+            users[d].append(i)
+    left, order = [len(c["deps"]) for c in calls], []
+    ready = [i for i in range(n) if left[i] == 0]
+    while ready:
+        i = min(ready, key=lambda j: (turn[j], j))
+        ready.remove(i)
+        order.append(i)
+        for j in users[i]:
+            left[j] -= 1
+            if left[j] == 0:
+                ready.append(j)
+    return order
 
 
 def rank_program(g, core, T, topo):
@@ -67,81 +115,58 @@ def rank_program(g, core, T, topo):
     nxt, prv = T.cores[(rank + 1) % n_ranks], T.cores[(rank - 1) % n_ranks]
     A, ACT = AluOpType, ActivationFunctionType
 
-    queue = {"v": g.vector, "a": g.scalar, "p": g.tensor, "g": g, "s": g.sync}
-    own = {"v": "cv", "a": "ca", "p": "cp", "g": "cg"}
-    total = {}
-    known = {q: {} for q in queue}
-    events = []
-    last_w, last_r = {}, {}
-    n_dma = [0]
+    calls, wrote, read = [], {}, {}
+    turns, now = {}, [None, None, None]
+    for period in range(R + 1):
+        for s in OPT["p%d" % period].split():
+            name, _, q = s.lstrip("<").partition(".")
+            turns[(period - s.count("<"), name)] = (len(turns), q)
 
-    def cols(view):
-        name, a, b, st = view
-        if name not in last_w:
-            last_w[name] = np.full(SCRATCH[name][1][1], -1)
-            last_r[name] = {}
-        if name == "ps":
-            return slice(a // 512 * 512, (b + 511) // 512 * 512)
-        return slice(a, b, st)
+    def step(period, name):
+        while (period, name) not in turns and period < R:
+            period += 1
+        now[0], now[1] = turns[(period, name)]
+        now[2] = (period, name)
 
-    def order(q, reads, writes):
-        deps = set()
+    def note(q, reads, writes, make, kind="c", after=(), adds=False):
+        i, deps, free = len(calls), set(after), set()
+        for vw in reads + writes:
+            if vw[0] not in wrote:
+                wrote[vw[0]], read[vw[0]] = np.full(SCRATCH[vw[0]][1][1], -1), {}
         for vw in reads:
-            s = cols(vw)
-            deps.update(last_w[vw[0]][s].tolist())
+            deps.update(wrote[vw[0]][cols(vw)].tolist())
             if vw[0] == "ps":
-                for sem, arr in last_r["ps"].items():
-                    if sem != own.get(q):
-                        deps.update(arr[s].tolist())
+                for q2, seen in read["ps"].items():
+                    if q2 != q:
+                        deps.update(j for j, s in seen if s == cols(vw))
         for vw in writes:
-            s = cols(vw)
-            deps.update(last_w[vw[0]][s].tolist())
-            for arr in last_r[vw[0]].values():
-                deps.update(arr[s].tolist())
+            hit = np.zeros(SCRATCH[vw[0]][1][1], bool)
+            hit[cols(vw)] = True
+            for q2, seen in read[vw[0]].items():
+                deps.update(j for j, s in seen if hit[s].any())
+                read[vw[0]][q2] = [(j, s) for j, s in seen if not hit[s].all()]
+            last = set(wrote[vw[0]][cols(vw)].tolist())
+            deps.update(last)
+            if adds:
+                free = last
         deps.discard(-1)
-        for e in sorted(deps, reverse=True):
-            sem, n, clock = events[e]
-            if known[q].get(sem, 0) < n:
-                queue[q].wait_ge(T.sem[sem], n)
-                for k2, v2 in clock.items():
-                    known[q][k2] = max(known[q].get(k2, 0), v2)
-
-    def done(q, sem, inc, reads, writes):
-        total[sem] = total.get(sem, 0) + inc
-        clock = dict(known[q]) if q else {}
-        clock[sem] = total[sem]
-        events.append((sem, total[sem], clock))
-        e = len(events) - 1
-        for vw in reads:
-            s = cols(vw)
-            if sem not in last_r[vw[0]]:
-                last_r[vw[0]][sem] = np.full(SCRATCH[vw[0]][1][1], -1)
-            last_r[vw[0]][sem][s] = e
         for vw in writes:
-            s = cols(vw)
-            last_w[vw[0]][s] = e
-
-    def call(q, reads, writes, make):
-        order(q, reads, writes)
-        make().then_inc(T.sem[own[q]], 1)
-        done(q, own[q], 1, reads, writes)
-
-    def dma(q, reads, writes, out, in_):
-        order(q, reads, writes)
-        sem = "d%d" % n_dma[0]
-        n_dma[0] += 1
-        queue[q].dma_start(out, in_).then_inc(T.sem[sem], 16)
-        done(q, sem, 16, reads, writes)
+            wrote[vw[0]][cols(vw)] = i
+        for vw in reads:
+            read[vw[0]].setdefault(q, []).append((i, cols(vw)))
+        calls.append(dict(q=q and q.lower(), make=make, kind=kind, deps=deps, free=free, turn=now[0] if q in ("v", "a", "G") else None, step=now[2]))
+        return i
 
     def V(name, a=0, b=None, st=1):
-        return (name, a, SCRATCH[name][1][1] if b is None else b, st)
+        host, at, n = PART.get(name) or (name, 0, SCRATCH[name][1][1])
+        return (host, at + a, at + (n if b is None else b), st)
 
     def ap(vw):
         name, a, b, st = vw
         return T[name][:, a:b] if st == 1 else T[name][:, a:b:st]
 
-    def bank(i, n):
-        return V("ps", 512 * i, 512 * i + n)
+    def bank(i, n, a=0):
+        return V("ps", 512 * i + a, 512 * i + n)
 
     def views(*xs):
         return [x for x in xs if isinstance(x, tuple)]
@@ -153,25 +178,25 @@ def rank_program(g, core, T, topo):
         return ap(x) if off is None else ap(x).indirect(ap(off))
 
     def memset(out, c):
-        call("v", [], [out], lambda: g.vector.memset(ap(out), c))
+        note("v", [], [out], lambda: g.vector.memset(ap(out), c))
 
-    def copy(out, in_, off=None):
-        call("v", views(in_, off), [out], lambda: g.vector.tensor_copy(ap(out), src(in_, off)))
+    def copy(out, in_):
+        note("v", [in_], [out], lambda: g.vector.tensor_copy(ap(out), ap(in_)))
 
     def scatter(win, off, in_):
-        call("v", [in_, off], [win], lambda: g.vector.tensor_copy(ap(win).indirect(ap(off)), ap(in_)))
+        note("v", [in_, off], [win], lambda: g.vector.tensor_copy(ap(win).indirect(ap(off)), ap(in_)))
 
     def tt(out, a, b, op, off=None):
-        call("v", views(a, b, off), [out], lambda: g.vector.tensor_tensor(ap(out), src(a, off), ap(b), op))
+        note("v", views(a, b, off), [out], lambda: g.vector.tensor_tensor(ap(out), src(a, off), ap(b), op))
 
     def ts(out, a, s1, op0, s2=None, op1=None, off=None):
         if op1 is None:
-            call("v", views(a, s1, off), [out], lambda: g.vector.tensor_scalar(ap(out), src(a, off), val(s1), None, op0))
+            note("v", views(a, s1, off), [out], lambda: g.vector.tensor_scalar(ap(out), src(a, off), val(s1), None, op0))
         else:
-            call("v", views(a, s1, s2, off), [out], lambda: g.vector.tensor_scalar(ap(out), src(a, off), val(s1), val(s2), op0, op1))
+            note("v", views(a, s1, s2, off), [out], lambda: g.vector.tensor_scalar(ap(out), src(a, off), val(s1), val(s2), op0, op1))
 
     def scan(out, d0, d1, init, op0, op1):
-        call("v", [d0, d1], [out], lambda: g.vector.tensor_tensor_scan(ap(out), ap(d0), ap(d1), init, op0, op1))
+        note("v", [d0, d1], [out], lambda: g.vector.tensor_tensor_scan(ap(out), ap(d0), ap(d1), init, op0, op1))
 
     def act(out, in_, func, off=None, bias=None, scale=None, acc=None):
         kw = {}
@@ -181,54 +206,56 @@ def rank_program(g, core, T, topo):
             kw["scale"] = val(scale)
         if acc is not None:
             kw["accum_out"] = ap(acc)
-        call("a", views(in_, off, bias, scale), views(out, acc), lambda: g.scalar.activation(ap(out), src(in_, off), func, **kw))
+        note("a", views(in_, off, bias, scale), views(out, acc), lambda: g.scalar.activation(ap(out), src(in_, off), func, **kw))
+
+    def move(out, in_, off=None, scale=None):
+        if now[1] == "a":
+            act(out, in_, ACT.Copy, off=off, scale=scale)
+        elif scale is None:
+            note("v", views(in_, off), [out], lambda: g.vector.tensor_copy(ap(out), src(in_, off)))
+        else:
+            ts(out, in_, scale, A.mult, off=off)
 
     def quant(pair, in_, a=0):
         n = (in_[2] - in_[1]) // 4
         c, s = V(pair + "c", a, a + n), V(pair + "s", a, a + n)
-        call("v", [in_], [c, s], lambda: g.vector.quantize_mx(ap(c), ap(s), ap(in_)))
+        note("v", [in_], [c, s], lambda: g.vector.quantize_mx(ap(c), ap(s), ap(in_)))
 
-    def mx(bk, w, a, x, start=True, stop=True):
-        n = C if x == "qy" else K
-        wc, ws, xc, xs = V(w + "c", a, a + 128), V(w + "s", a, a + 128), V(x + "c", 0, n), V(x + "s", 0, n)
-        out = bank(bk, xc[2])
-        call("p", [wc, ws, xc, xs], [out], lambda: g.tensor.matmul_mx(ap(out), ap(wc), ap(ws), ap(xc), ap(xs), start, stop))
+    def mx(bk, w, a, x, start=True, stop=True, x0=0, n=K, adds=False):
+        wc, ws, xc, xs = V(w + "c", a, a + 128), V(w + "s", a, a + 128), V(x + "c", x0, x0 + n), V(x + "s", x0, x0 + n)
+        out = bank(bk, n)
+        note("p", [wc, ws, xc, xs], [out], lambda: g.tensor.matmul_mx(ap(out), ap(wc), ap(ws), ap(xc), ap(xs), start, stop), adds=adds)
 
     def unpack(first, eye, x):
         for b in range(4):
             mx(first + b, eye, 128 * b, x)
 
-    def send(pair, land, dst, sem):
+    def count(out, pattern, base, by_partition=0):
+        note("G", [], [out], lambda: g.iota(ap(out), pattern, int(base), by_partition, allow_small_or_imprecise_dtypes=True))
+
+    def fill(out, c):
+        note("G", [V("cb", 0, 1)], [out], lambda: g.affine_select(ap(out), T.cb[:, 0:1], [[0, 1]], A.is_gt, c, 0, 0))
+
+    def dma(reads, writes, out, in_):
+        note("s", reads, writes, lambda: g.sync.dma_start(out, in_), "dma")
+
+    def message(pair, land, dst, frm, sem):
         rid, pid, _ = topo.addr(dst)
         m = topo.mask(core, dst)
-        order("g", [V(pair + "c"), V(pair + "s")], [])
-        eng = topo.engines(core, dst)
-        if FUSED:
-            n = len(eng) // 4
-            masks = [sum(1 << e for e in eng[i * n:i * n + n]) for i in range(4)]
-            to = [DstId(rid=rid, pnc=pid)]
-            ts_ = [RemoteDMATransfer(dst_ids=to, dma_engine_mask=masks[i], remote_sem=T.sem[sem],
-                                     src=T[pair + "c"][:, PC * i:PC * i + PC].bitcast(dt.uint8),
-                                     dst=T[land + "c"][:, PC * i:PC * i + PC].bitcast(dt.uint8)) for i in range(3)]
-            ts_.append(RemoteDMATransfer(dst_ids=to, dma_engine_mask=masks[3], remote_sem=T.sem[sem],
-                                         src=T[pair + "s"][:, 0:4 * PC], dst=T[land + "s"][:, 0:4 * PC]))
-            g.remote_dma_fused(ts_, local_sem=T.sem.sent)
-            total["sent"] = total.get("sent", 0) + len(eng)
-            return
-        g.remote_dma(T[land + "c"][:, 0:K].bitcast(dt.uint8), T[pair + "c"][:, 0:K].bitcast(dt.uint8), T.sem[sem], T.sem.sent, pid, rid, m)
-        g.remote_dma(T[land + "s"][:, 0:K], T[pair + "s"][:, 0:K], T.sem[sem], T.sem.sent, pid, rid, m)
-        total["sent"] = total.get("sent", 0) + 2 * len(eng)
 
-    def arrives(land, frm, sem):
-        done(None, sem, (1 if FUSED else 2) * len(topo.engines(frm, core)), [], [V(land + "c"), V(land + "s")])
+        def make():
+            g.remote_dma(T[land + "c"][:].bitcast(dt.uint8), T[pair + "c"][:].bitcast(dt.uint8), T.sem[sem], T.sem.sent, pid, rid, m)
+            g.remote_dma(T[land + "s"][:], T[pair + "s"][:], T.sem[sem], T.sem.sent, pid, rid, m)
+            return 2 * len(topo.engines(core, dst))
+        i = note("g", [V(pair + "c"), V(pair + "s")], [], make, "send")
+        note(None, [], [V(land + "c"), V(land + "s")], lambda: (sem, 2 * len(topo.engines(frm, core))), "land", [i])
 
-    def pad(pair):
-        if FUSED:
-            quant(pair, V("zero"), 128)
-
-    def unwrap(out, run, picked, n):
-        scan(V(run, 0, n), V("r01", 0, n), V(picked, 0, n), 0.0, A.mult, A.add)
-        ts(out, V(run, 15, n, 16), OFF, A.add)
+    def unwrap(period, names, out, k, table, off, n):
+        picked, run, ends = V("pick", C * k, C * k + n), V("run", C * k, C * k + n), V("run", C * k + 15, C * k + n, 16)
+        step(period, names[0]), tt(picked, table, V("mask", 0, n), A.mult, off=off)
+        step(period, names[1]), scan(run, V("r01", 0, n), picked, 0.0, A.mult, A.add)
+        step(period, names[2]), ts(out, ends, OFF, A.add)
+        return ends
 
     def plane(name, b, a, z):
         return V(name, C * b + a, C * b + z)
@@ -239,323 +266,300 @@ def rank_program(g, core, T, topo):
     def elem(name, b, n):
         return V(name, b, 4 * n, 4)
 
-    def evac(q, out, in_, c):
-        if q == "a":
-            act(out, in_, ACT.Copy, scale=c)
-        else:
-            ts(out, in_, c, A.mult)
+    def ones(n):
+        return V("one1", 0, n)
 
-    for r in range(R):
-        arrives("lm%d" % r, prv, "am%d" % r)
-        arrives("lh%d" % r, nxt, "ah%d" % r)
-
-    dma("s", [], [V("bdi")], T.bdi[:], T.bd[:])
-    dma("s", [], [V("xs", 0, 4 * K)], T.xs[:, 0:4 * K], T.x[:, 0:4 * K])
-    dma("s", [], [V("dsi")], T.dsi[:], T.ds[:])
-    dma("s", [], [V("xs", 4 * K, 4 * C)], T.xs[:, 4 * K:4 * C], T.x[:, 4 * K:4 * C])
-    call("g", [], [V("pint")], lambda: g.iota(T.pint[:], [[0, 2]], 0, 1))
-    memset(V("one1"), 1.0)
-    call("g", [V("one1")], [V("eye1")], lambda: g.affine_select(T.eye1[:], T.one1[:], [[-1, 520]], A.is_equal, 0.0, 3, 4))
-    call("g", [], [V("kint")], lambda: g.iota(T.kint[:], [[16, 16]], K + 16, 0, allow_small_or_imprecise_dtypes=True))
-    call("g", [], [V("uint")], lambda: g.iota(T.uint[:], [[16, 8]], 112, 0))
-    memset(V("ones"), 1.0)
-    memset(V("r01"), 1.0)
-    ts(V("pand"), V("pint"), 15, A.bitwise_and)
-    scan(V("iota"), V("ones"), V("ones"), -OFF - 1.0, A.mult, A.add)
-    memset(V("r01", 0, C, 16), 0.0)
-    copy(V("pcol"), V("pand"))
-    scan(V("jrow"), V("r01"), V("r01"), 0.0, A.mult, A.add)
-    memset(V("tau0", 0, C), 0.0)
-    ts(V("mask"), V("jrow"), V("pcol", 0, 1), A.is_equal)
+    dma([], [V("bdi")], T.bdi[:], T.bd[:])
+    dma([], [V("xs", 0, 4 * K)], T.xs[:, 0:4 * K], T.x[:, 0:4 * K])
+    dma([], [V("dsi")], T.dsi[:], T.ds[:])
+    dma([], [V("xs", 4 * K, 4 * C)], T.xs[:, 4 * K:4 * C], T.x[:, 4 * K:4 * C])
+    dma([V("xs")], [V("layc")], T.layc[:].bitcast(dt.uint8), T.wc[:])
+    dma([V("xs")], [V("lays")], T.lays[:], T.ws[:])
+    dma([V("xs")], [V("us")], T.us[:], T.u[:])
+    step(0, "first")
+    note("G", [], [V("pint")], lambda: g.iota(T.pint[:], [[0, 2]], 0, 1))
+    count(V("diag"), [[-1, 128]], 0, 1)
+    count(V("iota"), [[1, C]], -OFF)
+    count(V("jrow"), [[0, KW], [1, 16]], 0)
+    step(0, "eye0"), memset(V("eye1"), 0.0)
+    step(0, "tau0"), memset(V("tau0", 0, C), 0.0)
+    step(0, "pand"), ts(V("pand"), V("pint"), 15, A.bitwise_and)
+    step(0, "eye"), ts(V("eye1", 3, 515, 4), V("diag"), 0.0, A.is_equal)
+    step(0, "pcol"), copy(V("pcol"), V("pand"))
     for b in range(4):
-        quant("eq1", V("eye1", 3 - b, 515 - b), 128 * b)
-    if FUSED:
-        act(V("zero"), V("one1", 0, 512), ACT.Copy, scale=0.0)
-        pad("m0")
-    order("s", [V("xs")], [])
-    dma("s", [], [V("layc")], T.layc[:].bitcast(dt.uint8), T.wc[:])
-    dma("s", [], [V("lays")], T.lays[:], T.ws[:])
-    dma("s", [], [V("us")], T.us[:], T.u[:])
-    dma("s", [V("lh0c")], [V("vs")], T.vs[:], T.v[:])
+        step(0, "E%d" % b), quant("eq1", V("eye1", 3 - b, 515 - b), 128 * b)
+    step(0, "r01"), act(V("r01", 0, K), V("jrow"), ACT.Sign)
+    step(0, "mask")
+    if now[1] == "a":
+        act(V("mask", K, C), V("jrow"), ACT.Abs, scale=-1.0, bias=V("pcol", 0, 1))
+        act(V("mask", 0, K), V("mask", K, C), ACT.Relu, scale=-1.0, bias=1.0)
+    else:
+        ts(V("mask", 0, K), V("jrow"), V("pcol", 0, 1), A.is_equal)
+    step(0, "wide"), move(V("r01", K, C), V("r01", 0, K)), move(V("mask", K, C), V("mask", 0, K))
+    step(0, "early")
+    if 1 in OPT["slot"]:
+        count(V("tini"), [[C, 2], [1, K]], -OFF)
+    note("G", [], [V("uint")], lambda: g.iota(T.uint[:], [[16, 8]], 112, 0))
+    count(V("kint"), [[16, 16]], K + 16 - 128)
+    count(V("tau1", 0, C), [[1, C]], -OFF)
+    step(0, "uoff"), ts(V("uand"), V("uint"), 127, A.bitwise_and), copy(V("uoff"), V("uand"))
+    step(0, "rneg"), act(V("rneg"), V("r01", 0, K), ACT.Copy, scale=3 * BIG, bias=-3 * BIG)
+    step(0, "neg"), act(V("neg"), V("mask", 0, K), ACT.Copy, scale=BIG, bias=-BIG)
+    step(0, "kk"), ts(V("kkb"), V("kint"), V("pcol", 0, 1), A.add, 1.0 / 128, A.mult)
+    step(0, "late0")
+    count(V("tau2", 0, C), [[1, C]], -OFF)
+    count(V("offc"), [[0, 2]], OFF)
+    if any(OPT["pe"]):
+        for t in range(3):
+            count(V("fl", 4 * K * t, 4 * K * t + 4 * K), [[0, 4 * K]], 0)
+    step(0, "late1")
+    count(V("tau3", 0, C), [[1, C]], -OFF)
+    if any(OPT["pe"]):
+        count(V("port"), [[1, K]], K)
+        count(ones(512), [[0, 512]], 1)
+        note("G", [ones(512)], [V("blk1")], lambda: g.affine_select(T.blk1[:], T.one1[:, 0:512], [[-16, 8], [0, 64]], A.is_ge, 0.0, 0, 1))
+        note("G", [V("blk1")], [V("blk2")], lambda: g.affine_select(T.blk2[:], T.blk1[:], [[16, 8], [0, 64]], A.is_ge, 0.0, 15, -1))
+        count(V("arow", 0, 15), [[0, 15]], 0), count(V("arow", 15, 16), [[0, 1]], -DROP), count(V("arow", 16, K), [[0, K - 16]], 0)
+        count(V("cb", 0, 1), [[0, 1]], 0)
+        for c in range(1, KW):
+            fill(V("cb", c, c + 1), -DROP / (16 * c))
+        step(0, "bk"), quant("bk", V("blk2"))
+        step(0, "tab"), tt(V("tab"), V("port"), V("neg"), A.add)
+        for t in range(1, 3):
+            step(0, "qf%d" % t), quant("qf", V("fl", 4 * K * t, 4 * K * t + 4 * K), K * t)
+    step(0, "qu"), quant("qu", V("us"))
+    step(0, "pc"), note("v", [V("quc"), V("uoff")], [V("qpc")], lambda: g.vector.tensor_copy(
+        T.qpc[:, 0:128].bitcast(dt.uint32), T.quc[:, 0:128].bitcast(dt.uint32).indirect(T.uoff[:, 0:8])))
+    step(0, "ps"), note("a", [V("qus"), V("uoff")], [V("qps")], lambda: g.scalar.activation(
+        T.qps[:, 0:128], T.qus[:, 0:128].indirect(T.uoff[:, 0:8]), ACT.Copy))
 
-    act(V("tini", 0, K), V("iota", 0, K), ACT.Copy)
-    act(V("tini", K, C), V("iota", K, C), ACT.Copy, bias=float(K))
-    act(V("offc"), V("one1", 0, 2), ACT.Copy, scale=OFF)
-    act(V("rneg"), V("r01", 0, K), ACT.Copy, scale=3 * BIG, bias=-3 * BIG)
-    act(V("neg"), V("mask", 0, K), ACT.Copy, scale=BIG, bias=-BIG)
-    act(V("kk16"), V("kint"), ACT.Identity, bias=V("pcol", 0, 1))
-    for name, nd in (("kkb", ND), ("kkl", ND_LAST)):
-        act(V(name, 0, KW - nd), V("kk16", 0, KW - nd), ACT.Copy, scale=1.0 / TINY)
-        act(V(name, KW - nd, 16), V("kk16", KW - nd, 16), ACT.Copy)
-
-    def later_constants():
-        ts(V("uand"), V("uint"), 127, A.bitwise_and)
-        copy(V("uoff"), V("uand"))
-        for name in ("hh0", "m1", "hh1", "m2", "hh2"):
-            pad(name)
-
-    copy(V("bdw"), V("bdi"))
-    scatter(V("tau0", 0, C), V("bdw", 0, KW), V("iota", 0, K))
-    quant("ql", V("xs", 0, 4 * K))
-    unpack(4, "eq1", "ql")
-    copy(V("tw0"), V("dsi"))
-    scatter(V("tau0", 0, C), V("bdw", KW, 2 * KW), V("iota", K, C))
-    for b in range(4):
-        evac("a", plane("fh0", b, 0, K), bank(4 + b, K), 0.5)
-    quant("qh", V("xs", 4 * K, 4 * C))
-    unpack(0, "eq1", "qh")
-    tt(V("pick", 0, K), V("tau0", K, C), V("mask", 0, K), A.mult)
-    act(V("wtab"), V("tau0", 0, C), ACT.Copy, off=V("tw0"))
-    scan(V("run", 0, K), V("r01", 0, K), V("pick", 0, K), 0.0, A.mult, A.add)
-    evac("v", plane("fh0", 0, K, C), bank(0, K), 0.5)
-    ts(V("al0", KW, 2 * KW), V("run", 15, K, 16), OFF, A.add)
-    evac("a", plane("fh0", 1, K, C), bank(1, K), 0.5)
+    step(0, "bd"), copy(V("bdw"), V("bdi"))
+    step(0, "ds"), copy(V("tw0"), V("dsi"))
+    step(0, "sc"), scatter(V("tau0", 0, C), V("bdw"), V("iota"))
+    for h in range(2 if OPT["slot"] else 0):
+        step(0, "w%d" % h), move(V("wtab", K * h, K * h + K), V("tau0", 0, C), off=V("tw0", KW * h, KW * h + KW))
+    for h, pair in enumerate(("ql", "qh")):
+        step(0, "Q%d" % h), quant(pair, V("xs", 4 * K * h, 4 * K * h + 4 * K))
+        unpack(4 - 4 * h, "eq1", pair)
+        for b in range(4):
+            step(0, "F%d" % (4 * h + b)), move(plane("fh0", b, K * h, K * h + K), bank(4 - 4 * h + b, K), scale=0.5)
+    unwrap(0, ("hp", "hs", "hi"), V("al0", KW, 2 * KW), 3, V("tau0", K, C), None, K)
+    step(0, "trep0"), move(V("trep0"), V("tini" if 1 in OPT["slot"] else "iota"), off=V("tw0"))
 
     def make_m(r):
-        fh, al = "fh%d" % r, "al%d" % r
-        hi = V(al, KW, 2 * KW)
-        tau, lo, h = "tau%d" % r, V(al, 0, KW), K // 2
-        tt(V("pick2", 0, h), V(tau, 0, h), V("mask", 0, h), A.mult)
-        tt(V("pick", 0, K), V("wtab"), V("mask", 0, K), A.mult, off=hi)
-        tt(V("pick2", h, K), V(tau, h, K), V("mask", h, K), A.mult)
-        scan(V("run", 0, K), V("r01", 0, K), V("pick", 0, K), 0.0, A.mult, A.add)
-        scan(V("run2", 0, K), V("r01", 0, K), V("pick2", 0, K), 0.0, A.mult, A.add)
-        ts(V("bhi"), V("run", 15, K, 16), OFF, A.add)
-        for b in range(2):
-            ts(V("lo4", KW * b, KW * b + KW), V("run2", 15, K, 16), 4.0, A.mult, 4 * OFF + b, A.add)
+        fh, hi, lo = "fh%d" % r, V("al%d" % r, KW, 2 * KW), V("al%d" % r, 0, KW)
+        unwrap(r, ("lp", "ls", "lo"), lo, 1, V("tau%d" % r, 0, K), None, K)
+        by_slot = r in OPT["slot"]
+        unwrap(r, ("bp", "bs", "bhi"), V("bhi"), 0, V("wtab" if by_slot else "trep%d" % r), hi, K)
         for b in range(4):
-            if r > 0 and b >= MID:
-                evac("a", plane(fh, b, K, C), bank(b, K), 0.5)
-            if r == 0 and b == 1:
-                evac("a", plane(fh, 2, K, C), bank(2, K), 0.5)
-                evac("a", plane(fh, 3, K, C), bank(3, K), 0.5)
-            if False:
-                evac("a", plane(fh, b, K, C), bank(b, K), 0.5)
-            if r == 0 or b >= AMID:
-                act(quarter("ahi", b), plane(fh, b, 0, C), ACT.Copy, off=hi)
+            step(r, "a%d" % b), move(plane("fp", b, K, C), plane(fh, b, 0, C), off=hi)
+            step(r, "y%d" % b), move(plane("fp", b, 0, K), plane(fh, b, 0, C), off=lo)
+            if by_slot:
+                step(r, "m%d" % b), tt(elem("mt", b, K), plane(fh, b, 0, C), plane("fp", b, K, C), A.add, off=V("bhi"))
+                continue
+            step(r, "A%d" % b), move(quarter("ahi", b), plane("fp", b, K, C))
+            step(r, "m%d" % b), tt(elem("mt", b, K), plane("fp", b, 0, C), quarter("ahi", b), A.add, off=V("bhi"))
+        step(r, "qm"), quant("m%d" % r, V("mt"))
+        message("m%d" % r, "lm%d" % r, nxt, prv, "am%d" % r)
+
+    def low_half(r):
+        ends = V("run", C + 15, C + K, 16)
         for b in range(4):
-            tt(elem("mt", b, K), plane(fh, b, 0, C), quarter("ahi", b), A.add, off=V("bhi"))
-        ts(lo, V("run2", 15, K, 16), OFF, A.add)
-        for b in range(2, 4):
-            ts(V("lo4", KW * b, KW * b + KW), V("run2", 15, K, 16), 4.0, A.mult, 4 * OFF + b, A.add)
-        quant("m%d" % r, V("mt"))
-        send("m%d" % r, "lm%d" % r, nxt, "am%d" % r)
-
-    def z_low(r, b):
-        out = elem("xt%d" % (r + 1), b, K) if r < R - 1 else plane("xp", b, 0, K)
-        tt(out, plane("fh%d" % r, b, 0, C), quarter("alo", b), A.add, off=V("blo"))
-
-    def while_m_flies(r):
-        fh, al = "fh%d" % r, "al%d" % r
-        lo = V(al, 0, KW)
-        xt = V("xs" if r == 0 else "xt%d" % r)
-        for b in range(XA):
-            act(elem("xg", b, K), xt, ACT.Copy, off=V("lo4", KW * b, KW * b + KW))
-        for b in range(XA, 4):
-            copy(elem("xg", b, K), xt, off=V("lo4", KW * b, KW * b + KW))
-        if BETA_FIRST:
-            tt(V("pick2", 0, K), V("wtab"), V("mask", 0, K), A.mult, off=lo)
-        quant("qg", V("xg"))
+            step(r, "l%d" % b), ts(V("lo4", KW * b, KW * b + KW), ends, 4.0, A.mult, 4 * OFF + b, A.add)
+            step(r, "g%d" % b), move(elem("xg", b, K), V("xs" if r == 0 else "xt%d" % r), off=V("lo4", KW * b, KW * b + KW))
+        step(r, "qg"), quant("qg", V("xg"))
         for b in range(4):
             mx(b, "eq1", 128 * b, "qg", True, False)
+        unwrap(r, ("zp", "zs", "blo"), V("blo"), 2, V("wtab" if r in OPT["slot"] else "trep%d" % r), V("al%d" % r, 0, KW), K)
         for b in range(4):
-            act(quarter("alo", b), plane(fh, b, 0, C), ACT.Copy, off=lo)
-        if not BETA_FIRST:
-            tt(V("pick2", 0, K), V("wtab"), V("mask", 0, K), A.mult, off=lo)
-        unwrap(V("blo"), "run2", "pick2", K)
-        if r == 0:
-            later_constants()
-            act(V("trep0"), V("tini"), ACT.Copy, off=V("tw0"))
-        for b in range(ZM):
-            z_low(r, b)
-        if r == 0:
-            quant("qu", V("us"))
-            call("v", [V("quc"), V("uoff")], [V("qpc")], lambda: g.vector.tensor_copy(
-                T.qpc[:, 0:128].bitcast(dt.uint32), T.quc[:, 0:128].bitcast(dt.uint32).indirect(T.uoff[:, 0:8])))
+            out = elem("xt%d" % (r + 1), b, K) if r < R - 1 else plane("xp", b, 0, K)
+            if r in OPT["slot"]:
+                step(r, "z%d" % b), tt(out, plane("fh%d" % r, b, 0, C), plane("fp", b, 0, K), A.add, off=V("blo"))
+                continue
+            step(r, "Y%d" % b), move(quarter("alo", b), plane("fp", b, 0, K))
+            step(r, "z%d" % b), tt(out, plane("fp", b, 0, C), quarter("alo", b), A.add, off=V("blo"))
 
     def reply(r):
         for b in range(4):
             mx(b, "eq1", 128 * b, "lm%d" % r, False, True)
         for b in range(4):
-            evac("av"[b % 2], elem("vt", b, K), bank(b, K), 0.5)
-        quant("qm", V("vt"))
-        if r == 0:
-            act(V("trep1"), V("trep0"), ACT.Copy, off=V("al0"))
-        if r == R - 1:
-            act(V("sig"), V("iota"), ACT.Copy, off=V("al2"))
+            step(r, "v%d" % b), move(elem("vt", b, K), bank(b, K), scale=0.5)
+        step(r, "qv"), quant("qm", V("vt"))
         unpack(4, "lay", "qm")
-        for b in range(ZM, ZG):
-            z_low(r, b)
         for b in range(4):
-            evac("av"[b % 2], elem("ht", b, K), bank(4 + b, K), 0.0078125)
-        quant("hh%d" % r, V("ht"))
-        send("hh%d" % r, "lh%d" % r, prv, "ah%d" % r)
+            step(r, "h%d" % b), move(elem("ht", b, K), bank(4 + b, K), scale=0.0078125)
+        step(r, "qh"), quant("hh%d" % r, V("ht"))
+        message("hh%d" % r, "lh%d" % r, prv, nxt, "ah%d" % r)
 
-    def while_h_flies(r):
-        al = "al%d" % r
-        for b in range(ZG, 4):
-            z_low(r, b)
+    def carry_over(r):
+        al = V("al%d" % r)
         if r == 0:
-            call("a", [V("qus"), V("uoff")], [V("qps")], lambda: g.scalar.activation(
-                T.qps[:, 0:128], T.qus[:, 0:128].indirect(T.uoff[:, 0:8]), ACT.Copy))
-        if r == R - 1:
-            act(V("sig2"), V("sig"), ACT.Copy, off=V("al1"))
-        act(V("tau%d" % (r + 1), 0, C), V("tini"), ACT.Copy)
+            dma([V("lh0c")], [V("vs")], T.vs[:], T.v[:])
         if r < R - 1:
-            quant("ql", V("xt%d" % (r + 1), 0, 4 * K))
-            unpack(4, "eq1", "ql")
+            if r + 1 in OPT["slot"]:
+                unwrap(r, ("tp", "ts", "tw"), V("tw%d" % (r + 1)), 3, V("trep%d" % r), al, C)
+            if r == 0 or r + 1 not in OPT["slot"]:
+                step(r, "tr"), move(V("trep%d" % (r + 1)), V("trep%d" % r), off=al)
+            step(r, "ql"), quant("ql", V("xt%d" % (r + 1), 0, 4 * K))
+            unpack(0, "eq1", "ql")
             for b in range(4):
-                evac("a", plane("fh%d" % (r + 1), b, 0, K), bank(4 + b, K), 0.5)
-            tt(V("pick2"), V("trep%d" % r), V("mask"), A.mult, off=V(al))
-            unwrap(V("tw%d" % (r + 1)), "run2", "pick2", C)
+                step(r, "f%d" % b), move(plane("fh%d" % (r + 1), b, 0, K), bank(b, K), scale=0.5)
         else:
-            quant("qv", V("vs"))
-            tt(V("pick2"), V("sig2"), V("mask"), A.mult, off=V("bdw"))
-            scan(V("run2"), V("r01"), V("pick2"), 0.0, A.mult, A.add)
-            ts(V("porth"), V("run2", 15, C, 16), K - OFF, A.is_ge, float(K), A.mult)
-            ts(V("portw"), V("run2", 15, C, 16), OFF, A.add)
+            step(r, "sig"), move(V("sig"), V("iota"), off=al)
+            step(r, "sig2"), move(V("sig2"), V("sig"), off=V("al1"))
+            ends = unwrap(r, ("pp", "pn", "pw"), V("portw"), 3, V("sig2"), V("bdw"), C)
+            step(r, "ph"), ts(V("porth"), ends, K - OFF, A.is_ge, float(K), A.mult)
+            step(r, "pf"), tt(V("portf"), V("porth"), ends, A.add)
+            step(r, "ow"), ts(V("obw"), V("portf"), OFF, A.add)
+            step(r, "qV"), quant("qv", V("vs"))
 
-    def x_high(r, b):
-        out = V("xt%d" % (r + 1), 4 * K + b, 4 * C, 4) if r < R - 1 else plane("xp", b, K, C)
-        tt(out, bank(b, K), elem("mt", b, K), A.add)
+    def places_by_products(p, hi):
+        def flags(row, a, z):
+            base = 4 * K * (row // 4) + row % 4
+            return V("fl", base + 4 * a, base + 4 * z - 3, 4)
 
-    def x_col(q, b):
-        if q == "a":
-            act(elem("xc", b, C), plane("xp", b, 0, C), ACT.Copy, off=V("portw"))
+        step(p, "pos")
+        if now[1] == "a":
+            act(V("sg"), bank(6, K), ACT.Sign)
+            act(flags(3, 0, K), V("sg"), ACT.Relu, scale=DROP / 16)
         else:
-            copy(elem("xc", b, C), plane("xp", b, 0, C), off=V("portw"))
+            ts(flags(3, 0, K), bank(4, K), 0.0, A.is_gt, DROP / 16, A.mult)
+        step(p, "nwt"), ts(V("nwt", 0, KW), V("ss", 15, K, 16), 0.0, A.is_le, -1.0, A.mult)
+        step(p, "wb"), tt(V("wb", 0, KW), V("cb", 0, KW), V("nwt", 0, KW), A.subtract)
+        step(p, "eq"), tt(flags(2, 1, K), bank(4, K, 1), V("ss", 0, K - 1), A.is_equal)
+        step(p, "z"), act(V("fl", 64 + 2, 4 * K, 64), V("iota", 0, KW - 1), ACT.Copy, scale=0.0)
+        for c in range(KW):
+            row, n = KW - 1 - c + (2 if c < KW - 2 else 0), 16 * c
+            step(p, "c%d" % c)
+            if now[1] == "a":
+                sg = V("rows", K * c, K * c + n + 16)
+                act(sg, bank(6, n + 16), ACT.Sign, scale=-1.0, bias=V("ss", n + 15, n + 16))
+                act(flags(row, 0, n + 16), sg, ACT.Relu, scale=-1.0)
+            else:
+                ts(flags(row, 0, n + 16), bank(4, n + 16), V("ss", n + 15, n + 16), A.is_gt)
+            if c > 0:
+                step(p, "r%d" % c), act(V("rest", K * c, K * c + n), flags(row, 0, n), ACT.Identity, scale=V("nwt", c, c + 1),
+                                        bias=V("wb", c, c + 1), acc=V("arow", n + 15, n + 16))
+        for t in range(3):
+            step(p, "q%d" % t), quant("qf", V("fl", 4 * K * t, 4 * K * t + (4 * K if t == 0 else 512)), K * t)
+            mx(5, "bk", 0, "qf", t == 0, t == 2, x0=K * t, adds=t > 0)
+        step(p, "min"), tt(V("col"), bank(5, K), V("tab"), A.min)
+        step(p, "scan"), scan(V("cnt"), V("col"), V("arow"), 0.0, A.max, A.add)
+        step(p, "hi"), ts(hi, V("cnt", 15, K, 16), DROP, A.add)
 
-    def rebind(r):
-        last = r == R - 1
-        na = KW - (ND_LAST if last else ND)
-        lh, fh = "lh%d" % r, "fh%d" % (r + 1)
-        sv, sa = bank(4, K), bank(5, K)
-        mx(4, "qp", 0, lh)
-        mx(0, "eq1", 0, lh)
-        mx(5, "qp", 0, lh)
-        for b in range(1, 4):
-            mx(b, "eq1", 128 * b, lh)
-
-        def own_score(c):
-            return V("ss", 16 * c + 15, 16 * c + 16)
+    def places_by_rows(p, hi):
+        na, mine = KW - OPT["nd"], V("ss", 15, K, 16)
+        step(p, "ne"), tt(V("eq"), bank(4, K), V("ss"), A.not_equal)
+        pos, keep = V("rows", 15 * ROW + 1, K * ROW, 16 * ROW), V("rows", 15 * ROW + 2, K * ROW, 16 * ROW)
+        step(p, "gt"), ts(pos, mine, 0.0, A.is_gt, 128.0 / TINY, A.mult)
+        step(p, "wt"), ts(V("wt", 0, KW), mine, 0.0, A.is_le, TINY, A.max)
+        step(p, "es"), scan(V("rows", 0, K * ROW, ROW), V("r01", 0, K), V("eq"), 0.0, A.mult, A.add)
+        step(p, "keep"), tt(keep, pos, V("kkb", 0, KW), A.mult)
 
         def row(c):
-            return V("rows", ROW * c, ROW * c + ROW)
-
-        def before(c):
-            out, in_ = V("rows", ROW * c, ROW * c + 16 * c + 16), V("ps", sv[1], sv[1] + 16 * c + 16)
+            own, wt, n, at = V("ss", 16 * c + 15, 16 * c + 16), V("wt", c, c + 1), 16 * c + 16, (16 * c + 15) * ROW - K
+            whole, head, tail = V("rows", at, at + K + 3), V("rows", at, at + n), V("rows", at + n, at + K)
             if c < na:
-                ts(out, in_, own_score(c), A.is_le)
-            else:
-                ts(out, in_, own_score(c), A.is_le, V("wt", c, c + 1), A.mult)
-
-        def after(c):
-            out = V("rows", ROW * c + 16 * c + 16, ROW * c + K)
-            if c == KW - 1:
+                step(p, "b%d" % c), ts(head, bank(4, n), own, A.is_le)
+                if c < KW - 1:
+                    step(p, "s%d" % c)
+                    if now[1] == "v":
+                        ts(tail, bank(4, K, n), own, A.is_lt)
+                    else:
+                        act(tail, bank(6, K, n), ACT.Sign, bias=own, scale=-1.0)
+                step(p, "n%d" % c), act(whole, whole, ACT.Relu, scale=wt, acc=V("sum", c, c + 1))
                 return
-            if c < na:
-                act(out, V("ps", sa[1] + 16 * c + 16, sa[2]), ACT.Sign, bias=own_score(c), scale=-1.0)
-            else:
-                ts(out, V("ps", sv[1] + 16 * c + 16, sv[2]), own_score(c), A.is_lt, V("wt", c, c + 1), A.mult)
+            step(p, "b%d" % c), ts(head, bank(4, n), own, A.is_le, wt, A.mult)
+            if c < KW - 1:
+                step(p, "s%d" % c), ts(tail, bank(4, K, n), own, A.is_lt, wt, A.mult)
+            step(p, "t%d" % c), ts(V("rows", at + K, at + K + 3), V("rows", at + K, at + K + 3), wt, A.mult)
+            step(p, "n%d" % c), note("v", [whole], [V("sum", c, c + 1)],
+                                     lambda: g.vector.tensor_reduce(ap(V("sum", c, c + 1)), ap(whole), AxisListType.X, A.add))
 
-        def count(c):
-            if c < na:
-                act(row(c), row(c), ACT.Relu, scale=V("wt", c, c + 1), acc=V("cnt", c, c + 1))
-            else:
-                call("v", [row(c)], [V("cnt", c, c + 1)], lambda: g.vector.tensor_reduce(T.cnt[:, c:c + 1], ap(row(c)), AxisListType.X, A.add))
+        for c in range(KW):
+            row(c)
+        step(p, "hi"), ts(hi, V("sum", 0, KW), -15.75, A.add)
 
-        mine = V("ss", 15, K, 16)
-        tt(V("sm"), sv, V("neg"), A.add)
-        x_high(r, 0)
-        scan(V("ss"), V("rneg"), V("sm"), 0.0, A.add, A.max)
-        for c in range(na):
-            after(c)
-        x_high(r, 1)
-        tt(V("eq"), sv, V("ss"), A.not_equal)
-        ts(V("pos", 0, KW), mine, 0.0, A.is_gt)
-        ts(V("wt", 0, KW), mine, 0.0, A.is_le, TINY, A.max)
-        before(0)
-        scan(V("es"), V("r01", 0, K), V("eq"), 0.0, A.mult, A.add)
-        tt(V("keep", 0, KW), V("pos", 0, KW), V("kkl" if last else "kkb", 0, KW), A.mult)
-        before(1)
-        before(2)
-        tt(V("rows", K, na * ROW, ROW), V("es", 15, 16 * na, 16), V("keep", 0, na), A.add)
-        before(3)
-        for c in range(na, KW):
-            ts(V("rows", ROW * c + K, ROW * c + ROW), V("es", 16 * c + 15, 16 * c + 16), V("wt", c, c + 1), A.mult, V("keep", c, c + 1), A.add)
+    def rebind(r):
+        last, p = r == R - 1, r + 1
+        lh, fh, hi, tau = "lh%d" % r, "fh%d" % p, V("al%d" % p, KW, 2 * KW), "tau%d" % p
+        mx(4, "qp", 0, lh)
+        if any(turns.get((p, s), (0, ""))[1] == "a" for s in ["pos"] + ["%s%d" % (x, c) for x in "cs" for c in range(KW)]):
+            mx(6, "qp", 0, lh)
+        unpack(0, "eq1", lh)
+        step(p, "sm"), tt(V("sm"), bank(4, K), V("neg"), A.add)
+        step(p, "ss"), scan(V("ss"), V("rneg"), V("sm"), 0.0, A.add, A.max)
+        (places_by_products if OPT["pe"][r] else places_by_rows)(p, hi)
+        step(p, "sc"), scatter(V(tau, 0, C), hi, V("iota", K, C))
+        for b in range(4):
+            out = V("xt%d" % p, 4 * K + b, 4 * C, 4) if not last else plane("xp", b, K, C)
+            step(p, "x%d" % b), tt(out, bank(b, K), elem("mt", b, K), A.add)
         if not last:
-            for c in range(4, XAT):
-                before(c)
-            x_high(r, 2)
-            x_high(r, 3)
-            before(XAT)
-            before(XAT + 1)
-            quant("qh", V("xt%d" % (r + 1), 4 * K, 4 * C))
+            step(p, "qx"), quant("qh", V("xt%d" % p, 4 * K, 4 * C))
             unpack(0, "eq1", "qh")
-            for c in range(XAT + 2, KW):
-                before(c)
-            for c in range(na):
-                count(c)
-            for b in range(EARLY):
-                evac("a", plane(fh, b, K, C), bank(b, K), 0.5)
-        else:
-            x_col("a", 0)
-            x_col("a", 1)
-            x_high(r, 2)
-            x_high(r, 3)
-            for c in range(YPRE):
-                count(c)
-            if XCA == 3:
-                x_col("a", 2)
-            for c in range(4, XAT_LAST - 1):
-                before(c)
-            tt(V("portf"), V("porth"), V("run2", 15, C, 16), A.add)
-            if XCA == 2:
-                x_col("v", 2)
-            ts(V("obw"), V("portf"), OFF, A.add)
-            x_col("v", 3)
-            before(XAT_LAST - 1)
-            quant("qy", V("xc"))
-            mx(6, "qv", 0, "qy")
-            dma("s", [V("qyc")], [], T.oc[:], T.qyc[:].bitcast(dt.uint8))
-            for k in range(4):
-                dma("s", [V("qys")], [], T.osc[4 * k:4 * k + 4, :], T.qys[32 * k:32 * k + 4, :])
-            for c in range(XAT_LAST, KW):
-                before(c)
-            for c in range(YPRE, YAT):
-                count(c)
-            act(V("yt"), bank(6, C), ACT.Copy)
-            dma("s", [V("yt")], [], T.y[:], T.yt[:])
-            for c in range(YAT, na):
-                count(c)
-        for c in range(na, KW):
-            after(c)
-        for c in reversed(range(na, KW)):
-            count(c)
-        hi = V("al%d" % (r + 1), KW, 2 * KW)
-        tau = "tau%d" % (r + 1)
-        ts(hi, V("cnt", 0, KW), -15.75, A.add)
-        scatter(V(tau, 0, C), hi, V("iota", K, C))
-        act(V(tau, C, PL), V("iota"), ACT.Copy, off=hi)
-        if not last:
-            tw = "tw%d" % (r + 1)
-            for b in range(EARLY, MID):
-                evac("a", plane(fh, b, K, C), bank(b, K), 0.5)
-            for b in range(AMID):
-                act(quarter("ahi", b), plane(fh, b, 0, C), ACT.Copy, off=hi)
-            copy(V("wtab", 0, K), V(tau), off=V(tw, 0, KW))
-            act(V("wtab", K, C), V(tau), ACT.Copy, off=V(tw, KW, 2 * KW))
-        else:
-            ts(V("obr", 0, K), V(tau), OFF, A.add, off=V("obw", 0, KW))
-            act(V("obr", K, C), V(tau), ACT.Identity, off=V("obw", KW, 2 * KW), bias=V("offc", 0, 1))
-            dma("s", [V("obr")], [], T.ob[:], T.obr[0:128:16, :])
+            for b in range(4):
+                step(p, "e%d" % b), move(plane(fh, b, K, C), bank(b, K), scale=0.5)
+            if p in OPT["slot"]:
+                step(p, "tau"), move(V(tau, C, PL), V("iota"), off=hi)
+                for h in range(2):
+                    step(p, "w%d" % h), move(V("wtab", K * h, K * h + K), V(tau), off=V("tw%d" % p, KW * h, KW * h + KW))
+            return
+        step(p, "tau"), move(V(tau, C, PL), V("iota"), off=hi)
+        parts = OPT["parts"]
+        n = C // parts
+        for h in range(parts):
+            a, z = n * h, n * h + n
+            for b in range(4):
+                step(p, "G%d" % (4 * h + b)), move(V("xc", 4 * a + b, 4 * z, 4), plane("xp", b, 0, C), off=V("portw", a // 16, z // 16))
+            step(p, "qy%d" % h), quant("qy", V("xc", 4 * a, 4 * z), a)
+            mx(7 - h, "qv", 0, "qy", x0=a, n=n)
+            dma([V("qyc", a, z)], [], T.oc[:, 4 * a:4 * z], T.qyc[:, a:z].bitcast(dt.uint8))
+            step(p, "yt%d" % h), move(V("yt", a, z), bank(7 - h, n), scale=1.0)
+            dma([V("yt", a, z)], [], T.y[:, a:z], T.yt[:, a:z])
+        for k in range(4):
+            dma([V("qys")], [], T.osc[4 * k:4 * k + 4, :], T.qys[32 * k:32 * k + 4, :])
+        step(p, "o0"), ts(V("obr", 0, K), V(tau), OFF, A.add, off=V("obw", 0, KW))
+        step(p, "o1"), act(V("obr", K, C), V(tau), ACT.Identity, off=V("obw", KW, 2 * KW), bias=V("offc", 0, 1))
+        dma([V("obr")], [], T.ob[:], T.obr[0:128:16, :])
 
     for r in range(R):
         make_m(r)
-        while_m_flies(r)
+        low_half(r)
         reply(r)
-        while_h_flies(r)
+        carry_over(r)
         rebind(r)
+
+    queue = {"v": g.vector, "a": g.scalar, "p": g.tensor, "g": g, "s": g.sync}
+    own = {"v": "cv", "a": "ca", "p": "cp", "g": "cg"}
+    total, known, event, n_dma = {}, {q: {} for q in queue}, {}, 0
+    order = deal(calls)
+    place = {i: k for k, i in enumerate(order)}
+    for i in order:
+        c = calls[i]
+        q = c["q"]
+        if c["kind"] == "land":
+            sem, inc = c["make"]()
+            total[sem] = inc
+            event[i] = (sem, inc, {sem: inc})
+            continue
+        for d in sorted(c["deps"] - c["free"], key=lambda j: -place[j]):
+            sem, n, clock = event[d]
+            if known[q].get(sem, 0) < n:
+                queue[q].wait_ge(T.sem[sem], n)
+                for k2, v2 in clock.items():
+                    known[q][k2] = max(known[q].get(k2, 0), v2)
+        if c["kind"] == "send":
+            total["sent"] = total.get("sent", 0) + c["make"]()
+            continue
+        sem, inc = own.get(q), 1
+        if c["kind"] == "dma":
+            sem, inc = "d%d" % n_dma, 16
+            n_dma += 1
+        c["make"]().then_inc(T.sem[sem], inc)
+        total[sem] = total.get(sem, 0) + inc
+        clock = dict(known[q])
+        clock[sem] = total[sem]
+        event[i] = (sem, total[sem], clock)
 
     for sem, n in total.items():
         if known["g"].get(sem, 0) < n:

import numpy as np
from concourse.mybir import dt, AluOpType, AxisListType, ActivationFunctionType

C, K, R = 320, 160, 3
KW = K // 16
PL = C + K
OFF = 240.0
BIG = 1.0e29
DROP = 512.0
ROW = K + 4
TINY = 2.0 ** -20
Q4, U8, BF, F32, I32, U16 = "float8_e4m3fn_x4", "uint8", "bfloat16", "float32", "int32", "uint16"

PLACES = ("sm x0 ss s1.a s3.a s2.a s0.a x1 ne gt s6.a wt b0 s5.a s4.a es keep n0 b2 n2 b8 b1 n1 x3 b3 n3 s8.v n8 b4 n4 b7 b5 n5 x2 t9 b6 n6 "
          "s7.v b9 n7 qx e0.a n9 hi tau.a e1.a sc w1.a w0.v lp bp ls e3.a a0.a bs e2.a l0 a1.a l1 bhi a2.a lo m0 a3.a m1 m2 g0.a m3 l3 g1.a l2 "
          "y0.a qm g2.a y2.a g3.v zp qg y1.a zs blo z0 z1 ")
OPT = dict(
    pe=(False, False, True), nd=1, parts=1, slot=(0, 1, 2),
    p0="eye0 first pand tau0 pcol mask.a r01 eye E3 E0 bd E2 sc ds w0.a w1.a Q0 F0.a F3.a E1 hp Q1 hs hi F2.v F4.a F1.a bp a0.a F5.v bs F6.a "
       "a2.a early F7.v a3.a bhi a1.v m0 m1 trep0.a m2 m3 qm lp uoff neg ls lo l1 l2 l3 g2.a l0 g1.v g3.v g0.a y1.a y0.a zp y3.a qg zs blo qu "
       "y2.a z1 z0 v0.a v1.v v2.a v3.v qv h0.a h2.a z2 z3 ps wide.a tr.a rneg h1.v h3.v qh late0 pc ql f0.a f1.a f2.a f3.a tp kk ts tw",
    p1=PLACES + "v0.a v1.v v2.a v3.v y3.a qv h0.a h2.a qf2 z2 h1.v h3.v qh z3 ql f0.a f2.a tp f1.a qf1 f3.a ts tw late1",
    p2=PLACES + "sig.a v0.a v1.v v2.a v3.v y3.a sig2.a qv h0.a z3 h2.a z2 h1.v h3.v qh pp tab pn bk ph pw pf qV ow",
    p3="x2 G2.a sm x3 G3.a x1 ss pos.v x0 G0.a eq z c1.v G1.a c0.v nwt c6.v c9.v wb r6 r9 c4.v c5.v c3.v r3 c8.v r1 c2.v r2 c7.v r7 r5 q0 r8 r4 "
       "q1 q2 qy0 yt0.a min scan hi sc tau.a o0 o1")

SCRATCH = {"ps": ("psum", [128, 4096], F32)}


def _sb(name, n, dtype):
    SCRATCH[name] = ("sbuf", [128, n], dtype)


PART = {}


def _shared(host, n, dtype, names):
    for k, name in enumerate(names.split()):
        PART[name] = (host, n * k, n)
    _sb(host, n * len(names.split()), dtype)


def _pair(name, n):
    _sb(name + "c", n, Q4)
    _sb(name + "s", n, U8)


_sb("one1", 520, BF), _sb("eye1", 520, BF), _sb("blk1", 512, BF), _sb("blk2", 512, BF)
_pair("eq1", 512), _pair("bk", 128)
_sb("pint", 2, I32), _sb("pand", 2, I32), _sb("pcol", 2, F32), _sb("diag", 128, BF), _sb("iota", C, BF), _sb("r01", C, BF)
_sb("jrow", K, BF), _sb("wtab", C, BF), _sb("mask", C, BF), _sb("neg", K, F32), _sb("rneg", K, F32), _sb("port", K, F32), _sb("tab", K, F32), _sb("cb", 16, F32)
_sb("uint", 8, I32), _sb("uand", 8, I32), _sb("uoff", 8, U16), _sb("offc", 2, F32)
_sb("xs", 4 * C, BF), _sb("us", 512, BF), _sb("vs", 512, BF), _sb("bdi", 20, I32), _sb("dsi", 20, I32)
_pair("lay", 512), _pair("qu", 128), _pair("qp", 128), _pair("qv", 128), _pair("qy", C)
_sb("bdw", 20, U16), _sb("pick", 4 * C, BF), _sb("run", 4 * C, BF)
_sb("bhi", KW, U16), _sb("blo", KW, U16), _sb("sig", C, BF), _sb("sig2", C, BF), _sb("portf", 20, F32), _sb("porth", 20, F32)
_sb("portw", 20, U16), _sb("obw", 20, U16), _sb("obr", C, F32), _sb("tw0", 20, U16), _sb("tw1", 20, U16), _sb("tw2", 20, U16), _sb("tini", C, BF)
for _r in range(R + 1):
    _sb("tau%d" % _r, PL, BF), _sb("al%d" % _r, 20, U16)
for _r in range(R):
    _sb("trep%d" % _r, C, BF)
_shared("score", K, F32, "sm ss col cnt sg arow"), _shared("few", 16, F32, "nwt wb sum wt"), _sb("eq", K, BF)
_sb("fl", 12 * K, BF), _pair("qf", 3 * K), _sb("rest", KW * K, F32), _sb("rows", K * ROW, BF)
_shared("kk", 16, F32, "kint kkb")
_sb("fp", 4 * C, BF), _sb("alo", 4 * K, BF), _sb("ahi", 4 * K, BF), _sb("mt", 4 * K, BF), _sb("vt", 4 * K, BF), _sb("ht", 4 * K, BF), _sb("xg", 4 * K, BF)
_sb("xt1", 4 * C, BF), _sb("xt2", 4 * C, BF), _sb("lo4", 4 * KW, U16), _pair("qg", K)
_sb("xp", 4 * C, BF), _sb("xc", 4 * C, BF), _sb("yt", C, F32)
for _r in range(R):
    _sb("fh%d" % _r, 4 * C, BF)
    for _n in ("m", "lm", "hh", "lh"):
        _pair("%s%d" % (_n, _r), K)
_pair("qm", K), _pair("ql", K), _pair("qh", K)

SEMAPHORES = (["cv", "ca", "cp", "cg", "sent"] + ["am%d" % r for r in range(R)] + ["ah%d" % r for r in range(R)]
              + ["d%d" % i for i in range(24)])


def cols(view):
    name, a, b, st = view
    if name == "ps":
        return slice(a // 512 * 512, (b + 511) // 512 * 512)
    return slice(a, b, st)


def deal(calls):
    n = len(calls)
    turn = [c["turn"] for c in calls]
    for i, c in enumerate(calls):
        if turn[i] is None and c["q"] in ("s", "g", "p") and not any(calls[d]["kind"] == "land" for d in c["deps"] if c["q"] == "p"):
            turn[i] = max([turn[d] for d in c["deps"] if turn[d] is not None] + [-1])
    users = [[] for _ in calls]
    for i in reversed(range(n)):
        if turn[i] is None:
            turn[i] = min([turn[j] for j in users[i]])
        for d in calls[i]["deps"]:
            users[d].append(i)
    left, order = [len(c["deps"]) for c in calls], []
    ready = [i for i in range(n) if left[i] == 0]
    while ready:
        i = min(ready, key=lambda j: (turn[j], j))
        ready.remove(i)
        order.append(i)
        for j in users[i]:
            left[j] -= 1
            if left[j] == 0:
                ready.append(j)
    return order


def rank_program(g, core, T, topo):
    rank = T.rank_of(core)
    if rank is None:
        return
    n_ranks = len(T.cores)
    nxt, prv = T.cores[(rank + 1) % n_ranks], T.cores[(rank - 1) % n_ranks]
    A, ACT = AluOpType, ActivationFunctionType

    calls, wrote, read = [], {}, {}
    turns, now = {}, [None, None, None]
    for period in range(R + 1):
        for s in OPT["p%d" % period].split():
            name, _, q = s.lstrip("<").partition(".")
            turns[(period - s.count("<"), name)] = (len(turns), q)

    def step(period, name):
        while (period, name) not in turns and period < R:
            period += 1
        now[0], now[1] = turns[(period, name)]
        now[2] = (period, name)

    def note(q, reads, writes, make, kind="c", after=(), adds=False):
        i, deps, free = len(calls), set(after), set()
        for vw in reads + writes:
            if vw[0] not in wrote:
                wrote[vw[0]], read[vw[0]] = np.full(SCRATCH[vw[0]][1][1], -1), {}
        for vw in reads:
            deps.update(wrote[vw[0]][cols(vw)].tolist())
            if vw[0] == "ps":
                for q2, seen in read["ps"].items():
                    if q2 != q:
                        deps.update(j for j, s in seen if s == cols(vw))
        for vw in writes:
            hit = np.zeros(SCRATCH[vw[0]][1][1], bool)
            hit[cols(vw)] = True
            for q2, seen in read[vw[0]].items():
                deps.update(j for j, s in seen if hit[s].any())
                read[vw[0]][q2] = [(j, s) for j, s in seen if not hit[s].all()]
            last = set(wrote[vw[0]][cols(vw)].tolist())
            deps.update(last)
            if adds:
                free = last
        deps.discard(-1)
        for vw in writes:
            wrote[vw[0]][cols(vw)] = i
        for vw in reads:
            read[vw[0]].setdefault(q, []).append((i, cols(vw)))
        calls.append(dict(q=q and q.lower(), make=make, kind=kind, deps=deps, free=free, turn=now[0] if q in ("v", "a", "G") else None, step=now[2]))
        return i

    def V(name, a=0, b=None, st=1):
        host, at, n = PART.get(name) or (name, 0, SCRATCH[name][1][1])
        return (host, at + a, at + (n if b is None else b), st)

    def ap(vw):
        name, a, b, st = vw
        return T[name][:, a:b] if st == 1 else T[name][:, a:b:st]

    def bank(i, n, a=0):
        return V("ps", 512 * i + a, 512 * i + n)

    def views(*xs):
        return [x for x in xs if isinstance(x, tuple)]

    def val(x):
        return ap(x) if isinstance(x, tuple) else x

    def src(x, off):
        return ap(x) if off is None else ap(x).indirect(ap(off))

    def memset(out, c):
        note("v", [], [out], lambda: g.vector.memset(ap(out), c))

    def copy(out, in_):
        note("v", [in_], [out], lambda: g.vector.tensor_copy(ap(out), ap(in_)))

    def scatter(win, off, in_):
        note("v", [in_, off], [win], lambda: g.vector.tensor_copy(ap(win).indirect(ap(off)), ap(in_)))

    def tt(out, a, b, op, off=None):
        note("v", views(a, b, off), [out], lambda: g.vector.tensor_tensor(ap(out), src(a, off), ap(b), op))

    def ts(out, a, s1, op0, s2=None, op1=None, off=None):
        if op1 is None:
            note("v", views(a, s1, off), [out], lambda: g.vector.tensor_scalar(ap(out), src(a, off), val(s1), None, op0))
        else:
            note("v", views(a, s1, s2, off), [out], lambda: g.vector.tensor_scalar(ap(out), src(a, off), val(s1), val(s2), op0, op1))

    def scan(out, d0, d1, init, op0, op1):
        note("v", [d0, d1], [out], lambda: g.vector.tensor_tensor_scan(ap(out), ap(d0), ap(d1), init, op0, op1))

    def act(out, in_, func, off=None, bias=None, scale=None, acc=None):
        kw = {}
        if bias is not None:
            kw["bias"] = val(bias)
        if scale is not None:
            kw["scale"] = val(scale)
        if acc is not None:
            kw["accum_out"] = ap(acc)
        note("a", views(in_, off, bias, scale), views(out, acc), lambda: g.scalar.activation(ap(out), src(in_, off), func, **kw))

    def move(out, in_, off=None, scale=None):
        if now[1] == "a":
            act(out, in_, ACT.Copy, off=off, scale=scale)
        elif scale is None:
            note("v", views(in_, off), [out], lambda: g.vector.tensor_copy(ap(out), src(in_, off)))
        else:
            ts(out, in_, scale, A.mult, off=off)

    def quant(pair, in_, a=0):
        n = (in_[2] - in_[1]) // 4
        c, s = V(pair + "c", a, a + n), V(pair + "s", a, a + n)
        note("v", [in_], [c, s], lambda: g.vector.quantize_mx(ap(c), ap(s), ap(in_)))

    def mx(bk, w, a, x, start=True, stop=True, x0=0, n=K, adds=False):
        wc, ws, xc, xs = V(w + "c", a, a + 128), V(w + "s", a, a + 128), V(x + "c", x0, x0 + n), V(x + "s", x0, x0 + n)
        out = bank(bk, n)
        note("p", [wc, ws, xc, xs], [out], lambda: g.tensor.matmul_mx(ap(out), ap(wc), ap(ws), ap(xc), ap(xs), start, stop), adds=adds)

    def unpack(first, eye, x):
        for b in range(4):
            mx(first + b, eye, 128 * b, x)

    def count(out, pattern, base, by_partition=0):
        note("G", [], [out], lambda: g.iota(ap(out), pattern, int(base), by_partition, allow_small_or_imprecise_dtypes=True))

    def fill(out, c):
        note("G", [V("cb", 0, 1)], [out], lambda: g.affine_select(ap(out), T.cb[:, 0:1], [[0, 1]], A.is_gt, c, 0, 0))

    def dma(reads, writes, out, in_):
        note("s", reads, writes, lambda: g.sync.dma_start(out, in_), "dma")

    def message(pair, land, dst, frm, sem):
        rid, pid, _ = topo.addr(dst)
        m = topo.mask(core, dst)

        def make():
            g.remote_dma(T[land + "c"][:].bitcast(dt.uint8), T[pair + "c"][:].bitcast(dt.uint8), T.sem[sem], T.sem.sent, pid, rid, m)
            g.remote_dma(T[land + "s"][:], T[pair + "s"][:], T.sem[sem], T.sem.sent, pid, rid, m)
            return 2 * len(topo.engines(core, dst))
        i = note("g", [V(pair + "c"), V(pair + "s")], [], make, "send")
        note(None, [], [V(land + "c"), V(land + "s")], lambda: (sem, 2 * len(topo.engines(frm, core))), "land", [i])

    def unwrap(period, names, out, k, table, off, n):
        picked, run, ends = V("pick", C * k, C * k + n), V("run", C * k, C * k + n), V("run", C * k + 15, C * k + n, 16)
        step(period, names[0]), tt(picked, table, V("mask", 0, n), A.mult, off=off)
        step(period, names[1]), scan(run, V("r01", 0, n), picked, 0.0, A.mult, A.add)
        step(period, names[2]), ts(out, ends, OFF, A.add)
        return ends

    def plane(name, b, a, z):
        return V(name, C * b + a, C * b + z)

    def quarter(name, b):
        return V(name, K * b, K * b + K)

    def elem(name, b, n):
        return V(name, b, 4 * n, 4)

    def ones(n):
        return V("one1", 0, n)

    dma([], [V("bdi")], T.bdi[:], T.bd[:])
    dma([], [V("xs", 0, 4 * K)], T.xs[:, 0:4 * K], T.x[:, 0:4 * K])
    dma([], [V("dsi")], T.dsi[:], T.ds[:])
    dma([], [V("xs", 4 * K, 4 * C)], T.xs[:, 4 * K:4 * C], T.x[:, 4 * K:4 * C])
    dma([V("xs")], [V("layc")], T.layc[:].bitcast(dt.uint8), T.wc[:])
    dma([V("xs")], [V("lays")], T.lays[:], T.ws[:])
    dma([V("xs")], [V("us")], T.us[:], T.u[:])
    step(0, "first")
    note("G", [], [V("pint")], lambda: g.iota(T.pint[:], [[0, 2]], 0, 1))
    count(V("diag"), [[-1, 128]], 0, 1)
    count(V("iota"), [[1, C]], -OFF)
    count(V("jrow"), [[0, KW], [1, 16]], 0)
    step(0, "eye0"), memset(V("eye1"), 0.0)
    step(0, "tau0"), memset(V("tau0", 0, C), 0.0)
    step(0, "pand"), ts(V("pand"), V("pint"), 15, A.bitwise_and)
    step(0, "eye"), ts(V("eye1", 3, 515, 4), V("diag"), 0.0, A.is_equal)
    step(0, "pcol"), copy(V("pcol"), V("pand"))
    for b in range(4):
        step(0, "E%d" % b), quant("eq1", V("eye1", 3 - b, 515 - b), 128 * b)
    step(0, "r01"), act(V("r01", 0, K), V("jrow"), ACT.Sign)
    step(0, "mask")
    if now[1] == "a":
        act(V("mask", K, C), V("jrow"), ACT.Abs, scale=-1.0, bias=V("pcol", 0, 1))
        act(V("mask", 0, K), V("mask", K, C), ACT.Relu, scale=-1.0, bias=1.0)
    else:
        ts(V("mask", 0, K), V("jrow"), V("pcol", 0, 1), A.is_equal)
    step(0, "wide"), move(V("r01", K, C), V("r01", 0, K)), move(V("mask", K, C), V("mask", 0, K))
    step(0, "early")
    if 1 in OPT["slot"]:
        count(V("tini"), [[C, 2], [1, K]], -OFF)
    note("G", [], [V("uint")], lambda: g.iota(T.uint[:], [[16, 8]], 112, 0))
    count(V("kint"), [[16, 16]], K + 16 - 128)
    count(V("tau1", 0, C), [[1, C]], -OFF)
    step(0, "uoff"), ts(V("uand"), V("uint"), 127, A.bitwise_and), copy(V("uoff"), V("uand"))
    step(0, "rneg"), act(V("rneg"), V("r01", 0, K), ACT.Copy, scale=3 * BIG, bias=-3 * BIG)
    step(0, "neg"), act(V("neg"), V("mask", 0, K), ACT.Copy, scale=BIG, bias=-BIG)
    step(0, "kk"), ts(V("kkb"), V("kint"), V("pcol", 0, 1), A.add, 1.0 / 128, A.mult)
    step(0, "late0")
    count(V("tau2", 0, C), [[1, C]], -OFF)
    count(V("offc"), [[0, 2]], OFF)
    if any(OPT["pe"]):
        for t in range(3):
            count(V("fl", 4 * K * t, 4 * K * t + 4 * K), [[0, 4 * K]], 0)
    step(0, "late1")
    count(V("tau3", 0, C), [[1, C]], -OFF)
    if any(OPT["pe"]):
        count(V("port"), [[1, K]], K)
        count(ones(512), [[0, 512]], 1)
        note("G", [ones(512)], [V("blk1")], lambda: g.affine_select(T.blk1[:], T.one1[:, 0:512], [[-16, 8], [0, 64]], A.is_ge, 0.0, 0, 1))
        note("G", [V("blk1")], [V("blk2")], lambda: g.affine_select(T.blk2[:], T.blk1[:], [[16, 8], [0, 64]], A.is_ge, 0.0, 15, -1))
        count(V("arow", 0, 15), [[0, 15]], 0), count(V("arow", 15, 16), [[0, 1]], -DROP), count(V("arow", 16, K), [[0, K - 16]], 0)
        count(V("cb", 0, 1), [[0, 1]], 0)
        for c in range(1, KW):
            fill(V("cb", c, c + 1), -DROP / (16 * c))
        step(0, "bk"), quant("bk", V("blk2"))
        step(0, "tab"), tt(V("tab"), V("port"), V("neg"), A.add)
        for t in range(1, 3):
            step(0, "qf%d" % t), quant("qf", V("fl", 4 * K * t, 4 * K * t + 4 * K), K * t)
    step(0, "qu"), quant("qu", V("us"))
    step(0, "pc"), note("v", [V("quc"), V("uoff")], [V("qpc")], lambda: g.vector.tensor_copy(
        T.qpc[:, 0:128].bitcast(dt.uint32), T.quc[:, 0:128].bitcast(dt.uint32).indirect(T.uoff[:, 0:8])))
    step(0, "ps"), note("a", [V("qus"), V("uoff")], [V("qps")], lambda: g.scalar.activation(
        T.qps[:, 0:128], T.qus[:, 0:128].indirect(T.uoff[:, 0:8]), ACT.Copy))

    step(0, "bd"), copy(V("bdw"), V("bdi"))
    step(0, "ds"), copy(V("tw0"), V("dsi"))
    step(0, "sc"), scatter(V("tau0", 0, C), V("bdw"), V("iota"))
    for h in range(2 if OPT["slot"] else 0):
        step(0, "w%d" % h), move(V("wtab", K * h, K * h + K), V("tau0", 0, C), off=V("tw0", KW * h, KW * h + KW))
    for h, pair in enumerate(("ql", "qh")):
        step(0, "Q%d" % h), quant(pair, V("xs", 4 * K * h, 4 * K * h + 4 * K))
        unpack(4 - 4 * h, "eq1", pair)
        for b in range(4):
            step(0, "F%d" % (4 * h + b)), move(plane("fh0", b, K * h, K * h + K), bank(4 - 4 * h + b, K), scale=0.5)
    unwrap(0, ("hp", "hs", "hi"), V("al0", KW, 2 * KW), 3, V("tau0", K, C), None, K)
    step(0, "trep0"), move(V("trep0"), V("tini" if 1 in OPT["slot"] else "iota"), off=V("tw0"))

    def make_m(r):
        fh, hi, lo = "fh%d" % r, V("al%d" % r, KW, 2 * KW), V("al%d" % r, 0, KW)
        unwrap(r, ("lp", "ls", "lo"), lo, 1, V("tau%d" % r, 0, K), None, K)
        by_slot = r in OPT["slot"]
        unwrap(r, ("bp", "bs", "bhi"), V("bhi"), 0, V("wtab" if by_slot else "trep%d" % r), hi, K)
        for b in range(4):
            step(r, "a%d" % b), move(plane("fp", b, K, C), plane(fh, b, 0, C), off=hi)
            step(r, "y%d" % b), move(plane("fp", b, 0, K), plane(fh, b, 0, C), off=lo)
            if by_slot:
                step(r, "m%d" % b), tt(elem("mt", b, K), plane(fh, b, 0, C), plane("fp", b, K, C), A.add, off=V("bhi"))
                continue
            step(r, "A%d" % b), move(quarter("ahi", b), plane("fp", b, K, C))
            step(r, "m%d" % b), tt(elem("mt", b, K), plane("fp", b, 0, C), quarter("ahi", b), A.add, off=V("bhi"))
        step(r, "qm"), quant("m%d" % r, V("mt"))
        message("m%d" % r, "lm%d" % r, nxt, prv, "am%d" % r)

    def low_half(r):
        ends = V("run", C + 15, C + K, 16)
        for b in range(4):
            step(r, "l%d" % b), ts(V("lo4", KW * b, KW * b + KW), ends, 4.0, A.mult, 4 * OFF + b, A.add)
            step(r, "g%d" % b), move(elem("xg", b, K), V("xs" if r == 0 else "xt%d" % r), off=V("lo4", KW * b, KW * b + KW))
        step(r, "qg"), quant("qg", V("xg"))
        for b in range(4):
            mx(b, "eq1", 128 * b, "qg", True, False)
        unwrap(r, ("zp", "zs", "blo"), V("blo"), 2, V("wtab" if r in OPT["slot"] else "trep%d" % r), V("al%d" % r, 0, KW), K)
        for b in range(4):
            out = elem("xt%d" % (r + 1), b, K) if r < R - 1 else plane("xp", b, 0, K)
            if r in OPT["slot"]:
                step(r, "z%d" % b), tt(out, plane("fh%d" % r, b, 0, C), plane("fp", b, 0, K), A.add, off=V("blo"))
                continue
            step(r, "Y%d" % b), move(quarter("alo", b), plane("fp", b, 0, K))
            step(r, "z%d" % b), tt(out, plane("fp", b, 0, C), quarter("alo", b), A.add, off=V("blo"))

    def reply(r):
        for b in range(4):
            mx(b, "eq1", 128 * b, "lm%d" % r, False, True)
        for b in range(4):
            step(r, "v%d" % b), move(elem("vt", b, K), bank(b, K), scale=0.5)
        step(r, "qv"), quant("qm", V("vt"))
        unpack(4, "lay", "qm")
        for b in range(4):
            step(r, "h%d" % b), move(elem("ht", b, K), bank(4 + b, K), scale=0.0078125)
        step(r, "qh"), quant("hh%d" % r, V("ht"))
        message("hh%d" % r, "lh%d" % r, prv, nxt, "ah%d" % r)

    def carry_over(r):
        al = V("al%d" % r)
        if r == 0:
            dma([V("lh0c")], [V("vs")], T.vs[:], T.v[:])
        if r < R - 1:
            if r + 1 in OPT["slot"]:
                unwrap(r, ("tp", "ts", "tw"), V("tw%d" % (r + 1)), 3, V("trep%d" % r), al, C)
            if r == 0 or r + 1 not in OPT["slot"]:
                step(r, "tr"), move(V("trep%d" % (r + 1)), V("trep%d" % r), off=al)
            step(r, "ql"), quant("ql", V("xt%d" % (r + 1), 0, 4 * K))
            unpack(0, "eq1", "ql")
            for b in range(4):
                step(r, "f%d" % b), move(plane("fh%d" % (r + 1), b, 0, K), bank(b, K), scale=0.5)
        else:
            step(r, "sig"), move(V("sig"), V("iota"), off=al)
            step(r, "sig2"), move(V("sig2"), V("sig"), off=V("al1"))
            ends = unwrap(r, ("pp", "pn", "pw"), V("portw"), 3, V("sig2"), V("bdw"), C)
            step(r, "ph"), ts(V("porth"), ends, K - OFF, A.is_ge, float(K), A.mult)
            step(r, "pf"), tt(V("portf"), V("porth"), ends, A.add)
            step(r, "ow"), ts(V("obw"), V("portf"), OFF, A.add)
            step(r, "qV"), quant("qv", V("vs"))

    def places_by_products(p, hi):
        def flags(row, a, z):
            base = 4 * K * (row // 4) + row % 4
            return V("fl", base + 4 * a, base + 4 * z - 3, 4)

        step(p, "pos")
        if now[1] == "a":
            act(V("sg"), bank(6, K), ACT.Sign)
            act(flags(3, 0, K), V("sg"), ACT.Relu, scale=DROP / 16)
        else:
            ts(flags(3, 0, K), bank(4, K), 0.0, A.is_gt, DROP / 16, A.mult)
        step(p, "nwt"), ts(V("nwt", 0, KW), V("ss", 15, K, 16), 0.0, A.is_le, -1.0, A.mult)
        step(p, "wb"), tt(V("wb", 0, KW), V("cb", 0, KW), V("nwt", 0, KW), A.subtract)
        step(p, "eq"), tt(flags(2, 1, K), bank(4, K, 1), V("ss", 0, K - 1), A.is_equal)
        step(p, "z"), act(V("fl", 64 + 2, 4 * K, 64), V("iota", 0, KW - 1), ACT.Copy, scale=0.0)
        for c in range(KW):
            row, n = KW - 1 - c + (2 if c < KW - 2 else 0), 16 * c
            step(p, "c%d" % c)
            if now[1] == "a":
                sg = V("rows", K * c, K * c + n + 16)
                act(sg, bank(6, n + 16), ACT.Sign, scale=-1.0, bias=V("ss", n + 15, n + 16))
                act(flags(row, 0, n + 16), sg, ACT.Relu, scale=-1.0)
            else:
                ts(flags(row, 0, n + 16), bank(4, n + 16), V("ss", n + 15, n + 16), A.is_gt)
            if c > 0:
                step(p, "r%d" % c), act(V("rest", K * c, K * c + n), flags(row, 0, n), ACT.Identity, scale=V("nwt", c, c + 1),
                                        bias=V("wb", c, c + 1), acc=V("arow", n + 15, n + 16))
        for t in range(3):
            step(p, "q%d" % t), quant("qf", V("fl", 4 * K * t, 4 * K * t + (4 * K if t == 0 else 512)), K * t)
            mx(5, "bk", 0, "qf", t == 0, t == 2, x0=K * t, adds=t > 0)
        step(p, "min"), tt(V("col"), bank(5, K), V("tab"), A.min)
        step(p, "scan"), scan(V("cnt"), V("col"), V("arow"), 0.0, A.max, A.add)
        step(p, "hi"), ts(hi, V("cnt", 15, K, 16), DROP, A.add)

    def places_by_rows(p, hi):
        na, mine = KW - OPT["nd"], V("ss", 15, K, 16)
        step(p, "ne"), tt(V("eq"), bank(4, K), V("ss"), A.not_equal)
        pos, keep = V("rows", 15 * ROW + 1, K * ROW, 16 * ROW), V("rows", 15 * ROW + 2, K * ROW, 16 * ROW)
        step(p, "gt"), ts(pos, mine, 0.0, A.is_gt, 128.0 / TINY, A.mult)
        step(p, "wt"), ts(V("wt", 0, KW), mine, 0.0, A.is_le, TINY, A.max)
        step(p, "es"), scan(V("rows", 0, K * ROW, ROW), V("r01", 0, K), V("eq"), 0.0, A.mult, A.add)
        step(p, "keep"), tt(keep, pos, V("kkb", 0, KW), A.mult)

        def row(c):
            own, wt, n, at = V("ss", 16 * c + 15, 16 * c + 16), V("wt", c, c + 1), 16 * c + 16, (16 * c + 15) * ROW - K
            whole, head, tail = V("rows", at, at + K + 3), V("rows", at, at + n), V("rows", at + n, at + K)
            if c < na:
                step(p, "b%d" % c), ts(head, bank(4, n), own, A.is_le)
                if c < KW - 1:
                    step(p, "s%d" % c)
                    if now[1] == "v":
                        ts(tail, bank(4, K, n), own, A.is_lt)
                    else:
                        act(tail, bank(6, K, n), ACT.Sign, bias=own, scale=-1.0)
                step(p, "n%d" % c), act(whole, whole, ACT.Relu, scale=wt, acc=V("sum", c, c + 1))
                return
            step(p, "b%d" % c), ts(head, bank(4, n), own, A.is_le, wt, A.mult)
            if c < KW - 1:
                step(p, "s%d" % c), ts(tail, bank(4, K, n), own, A.is_lt, wt, A.mult)
            step(p, "t%d" % c), ts(V("rows", at + K, at + K + 3), V("rows", at + K, at + K + 3), wt, A.mult)
            step(p, "n%d" % c), note("v", [whole], [V("sum", c, c + 1)],
                                     lambda: g.vector.tensor_reduce(ap(V("sum", c, c + 1)), ap(whole), AxisListType.X, A.add))

        for c in range(KW):
            row(c)
        step(p, "hi"), ts(hi, V("sum", 0, KW), -15.75, A.add)

    def rebind(r):
        last, p = r == R - 1, r + 1
        lh, fh, hi, tau = "lh%d" % r, "fh%d" % p, V("al%d" % p, KW, 2 * KW), "tau%d" % p
        mx(4, "qp", 0, lh)
        if any(turns.get((p, s), (0, ""))[1] == "a" for s in ["pos"] + ["%s%d" % (x, c) for x in "cs" for c in range(KW)]):
            mx(6, "qp", 0, lh)
        unpack(0, "eq1", lh)
        step(p, "sm"), tt(V("sm"), bank(4, K), V("neg"), A.add)
        step(p, "ss"), scan(V("ss"), V("rneg"), V("sm"), 0.0, A.add, A.max)
        (places_by_products if OPT["pe"][r] else places_by_rows)(p, hi)
        step(p, "sc"), scatter(V(tau, 0, C), hi, V("iota", K, C))
        for b in range(4):
            out = V("xt%d" % p, 4 * K + b, 4 * C, 4) if not last else plane("xp", b, K, C)
            step(p, "x%d" % b), tt(out, bank(b, K), elem("mt", b, K), A.add)
        if not last:
            step(p, "qx"), quant("qh", V("xt%d" % p, 4 * K, 4 * C))
            unpack(0, "eq1", "qh")
            for b in range(4):
                step(p, "e%d" % b), move(plane(fh, b, K, C), bank(b, K), scale=0.5)
            if p in OPT["slot"]:
                step(p, "tau"), move(V(tau, C, PL), V("iota"), off=hi)
                for h in range(2):
                    step(p, "w%d" % h), move(V("wtab", K * h, K * h + K), V(tau), off=V("tw%d" % p, KW * h, KW * h + KW))
            return
        step(p, "tau"), move(V(tau, C, PL), V("iota"), off=hi)
        parts = OPT["parts"]
        n = C // parts
        for h in range(parts):
            a, z = n * h, n * h + n
            for b in range(4):
                step(p, "G%d" % (4 * h + b)), move(V("xc", 4 * a + b, 4 * z, 4), plane("xp", b, 0, C), off=V("portw", a // 16, z // 16))
            step(p, "qy%d" % h), quant("qy", V("xc", 4 * a, 4 * z), a)
            mx(7 - h, "qv", 0, "qy", x0=a, n=n)
            dma([V("qyc", a, z)], [], T.oc[:, 4 * a:4 * z], T.qyc[:, a:z].bitcast(dt.uint8))
            step(p, "yt%d" % h), move(V("yt", a, z), bank(7 - h, n), scale=1.0)
            dma([V("yt", a, z)], [], T.y[:, a:z], T.yt[:, a:z])
        for k in range(4):
            dma([V("qys")], [], T.osc[4 * k:4 * k + 4, :], T.qys[32 * k:32 * k + 4, :])
        step(p, "o0"), ts(V("obr", 0, K), V(tau), OFF, A.add, off=V("obw", 0, KW))
        step(p, "o1"), act(V("obr", K, C), V(tau), ACT.Identity, off=V("obw", KW, 2 * KW), bias=V("offc", 0, 1))
        dma([V("obr")], [], T.ob[:], T.obr[0:128:16, :])

    for r in range(R):
        make_m(r)
        low_half(r)
        reply(r)
        carry_over(r)
        rebind(r)

    queue = {"v": g.vector, "a": g.scalar, "p": g.tensor, "g": g, "s": g.sync}
    own = {"v": "cv", "a": "ca", "p": "cp", "g": "cg"}
    total, known, event, n_dma = {}, {q: {} for q in queue}, {}, 0
    order = deal(calls)
    place = {i: k for k, i in enumerate(order)}
    for i in order:
        c = calls[i]
        q = c["q"]
        if c["kind"] == "land":
            sem, inc = c["make"]()
            total[sem] = inc
            event[i] = (sem, inc, {sem: inc})
            continue
        for d in sorted(c["deps"] - c["free"], key=lambda j: -place[j]):
            sem, n, clock = event[d]
            if known[q].get(sem, 0) < n:
                queue[q].wait_ge(T.sem[sem], n)
                for k2, v2 in clock.items():
                    known[q][k2] = max(known[q].get(k2, 0), v2)
        if c["kind"] == "send":
            total["sent"] = total.get("sent", 0) + c["make"]()
            continue
        sem, inc = own.get(q), 1
        if c["kind"] == "dma":
            sem, inc = "d%d" % n_dma, 16
            n_dma += 1
        c["make"]().then_inc(T.sem[sem], inc)
        total[sem] = total.get(sem, 0) + inc
        clock = dict(known[q])
        clock[sem] = total[sem]
        event[i] = (sem, total[sem], clock)

    for sem, n in total.items():
        if known["g"].get(sem, 0) < n:
            g.wait_ge(T.sem[sem], n)
